import numpy as np
import ml_dtypes


def mxq(x, axis, fmt="e4m3"):
    dtype, down = {"e4m3": (ml_dtypes.float8_e4m3fn, 7), "e5m2": (ml_dtypes.float8_e5m2, 14)}[fmt]
    v = np.moveaxis(np.asarray(x, np.float32).astype(ml_dtypes.bfloat16).astype(np.float64), axis, -1)
    blocks = v.reshape(v.shape[:-1] + (-1, 32))
    amax = np.abs(blocks).max(-1, keepdims=True)
    byte = np.maximum(np.where(amax > 0, np.frexp(amax)[1] - 1 + 127, 0) - down, 1)
    scale = np.exp2(byte - 127.0)
    codes = (blocks / scale).astype(np.float32).astype(dtype).astype(np.float64)
    return np.moveaxis((codes * scale).reshape(v.shape), -1, axis)


WIDE = False


def mx_kscale(k):
    if not WIDE:
        return np.ones(k)
    levels = np.array([10, -10, 5, -5, 0])
    if k % 512:
        return np.exp2(np.random.permutation(np.resize(levels, k // 32))).repeat(32)
    a = np.empty((k // 512, 16))
    for p in range(k // 512):
        a[p, :8] = np.random.permutation(np.resize(levels, 8))
        for g in range(8):
            far = levels[np.abs(levels - a[p, g]) >= 10]
            a[p, g + 8] = far[np.random.randint(len(far))]
    return np.exp2(a.ravel()).repeat(32)


BF16 = ml_dtypes.bfloat16


def bf(x):
    return np.asarray(x, np.float32).astype(BF16)


def f64(x):
    return np.asarray(x).astype(np.float64)


N, K, P, H = 1024, 1536, 1024, 1024


def draw0():
    s = mx_kscale(K)
    r = mx_kscale(P)
    t = mx_kscale(P)
    return {
        "z": bf(np.random.standard_normal((N, K)) * s),
        "m": bf(np.random.standard_normal((N, P)) * r),
        "ez": bf(np.random.standard_normal(K) / np.sqrt(K) / s),
        "at": bf(np.random.standard_normal((P, P)) / np.sqrt(P) / r[:, None] * t),
        "bvec": bf(np.random.standard_normal(P) * 0.7 * t),
        "wz": bf(np.random.standard_normal((K, H)) * 0.7 / np.sqrt(K) / s[:, None]),
        "wm": bf(np.random.standard_normal((P, H)) * 0.7 / np.sqrt(P) / t[:, None]),
    }


def write_scalar(z, ez):
    return np.sum(z * ez[None, :], axis=-1)


def update_memory(m, u, at, bvec):
    a = mxq(m, 1, "e4m3") @ mxq(at, 0, "e4m3")
    return a + u[:, None] * bvec[None, :]


def core(z, m, ez, at, bvec, wz, wm):
    z, m = f64(z), f64(m)
    u = write_scalar(z, f64(ez))
    m_new = update_memory(m, u, f64(at), f64(bvec))
    s = (mxq(z, 1, "e4m3") @ mxq(f64(wz), 0, "e4m3")) + (mxq(m_new, 1, "e4m3") @ mxq(f64(wm), 0, "e4m3"))
    return np.tanh(s)


def e4m3fn_bytes(y):
    return np.clip(np.asarray(y, np.float64), -448.0, 448.0).astype(np.float32).astype(ml_dtypes.float8_e4m3fn).view(np.uint8)


def e4m3fn_values(b):
    return np.asarray(b, np.uint8).view(ml_dtypes.float8_e4m3fn).astype(np.float64)


def setup_inputs():
    d = draw0()
    x0 = np.asarray(d['wz']).astype(np.float64)
    s = (np.max(np.abs(x0), axis=(1,), keepdims=True) / 448.0).astype(np.float32)
    out = {}
    for k, v in d.items():
        if k == 'wz':
            out['wz_bytes'] = e4m3fn_bytes(x0 / s.astype(np.float64))
            out['wz_scale'] = s
        else:
            out[k] = v
    return out


def reference(z, m, ez, at, bvec, wz_bytes, wz_scale, wm):
    return core(z, m, ez, at, bvec, e4m3fn_values(wz_bytes) * wz_scale.astype(np.float64), wm)

@@ -1,0 +1,293 @@
+from contextlib import ExitStack
+
+import concourse.mybir as mybir
+from concourse.masks import make_identity
+
+N, K, P_MEM, H = 1024, 1536, 1024, 1024
+FLOPS = 2 * N * (K * H + P_MEM * P_MEM + P_MEM * H) + 2 * N * K + 3 * N * P_MEM
+
+F32 = mybir.dt.float32
+BF16 = mybir.dt.bfloat16
+U32 = mybir.dt.uint32
+U8 = mybir.dt.uint8
+FP8 = mybir.dt.float8_e4m3fn
+FP8X4 = mybir.dt.float8_e4m3fn_x4
+ACT = mybir.ActivationFunctionType
+ALU = mybir.AluOpType
+
+P = 128
+PACK = 4
+PASS = P * PACK
+W = 512
+ZG = K // PASS
+MG = P_MEM // PASS
+HALVES = N // W
+
+
+def tile_legendrememoryunitstep_kernel(tc, z, m, ez, at, bvec, wz_bytes, wz_scale, wm, out):
+    nc = tc.nc
+    with ExitStack() as ctx:
+        keep = ctx.enter_context(tc.tile_pool(name="keep", bufs=1))
+        raw = ctx.enter_context(tc.tile_pool(name="raw", bufs=1))
+        work = ctx.enter_context(tc.tile_pool(name="work", bufs=1))
+        psum = ctx.enter_context(tc.psum_pool(name="psum", bufs=1))
+        at_raw, m_raw, z_raw, wz_raw, wm_raw = {}, {}, {}, {}, {}
+        at_src = at.rearrange("(g p j) w -> g p j w", p=P, j=PACK)
+        wm_src = wm.rearrange("(g p j) w -> g p j w", p=P, j=PACK)
+        wz_src = wz_bytes.rearrange("(g p j) w -> g p j w", p=P, j=PACK)
+
+        def load_w(store, src, g, c):
+            t = raw.tile([P, PACK, W], BF16, name="w_raw", tag="w_raw", bufs=6)
+            nc.sync.dma_start(out=t[:], in_=src[g][:, :, c * W : (c + 1) * W])
+            store[g, c] = t
+
+        def load_m(i):
+            t = raw.tile([P, P_MEM], BF16, name="m_raw", tag="m_raw", bufs=6)
+            nc.sync.dma_start(out=t[:], in_=m[i * P : (i + 1) * P, :])
+            m_raw[i] = t
+
+        def load_z(i):
+            t = raw.tile([P, K], BF16, name="z_raw", tag="z_raw", bufs=7)
+            nc.sync.dma_start(out=t[:], in_=z[i * P : (i + 1) * P, :])
+            z_raw[i] = t
+
+        def load_wz(g):
+            t = raw.tile([P, PACK, H], U8, name="wz_codes_in", tag="wz_codes_in", bufs=3)
+            nc.sync.dma_start(out=t[:], in_=wz_src[g])
+            wz_raw[g] = t
+
+        warm = keep.tile([P, 1], F32, name="warm")
+        nc.vector.memset(warm[:], 0.0)
+        warm_out = keep.tile([P, 1], F32, name="warm_out")
+        nc.scalar.activation(out=warm_out[:], in_=warm[:], func=ACT.Tanh)
+        ident = keep.tile([P, P], F32, name="ident")
+        make_identity(nc, ident[:])
+        ez_sb = keep.tile([P, ZG, PACK], BF16, name="ez_sb")
+        bv_sb = keep.tile([P, MG, PACK], BF16, name="bv_sb")
+        sc_sb = keep.tile([P, ZG, PACK], F32, name="sc_sb")
+
+        def codes_tile(name):
+            c = keep.tile([P, W], U32, name=name, tag=name, align_bytes=64)
+            s = keep.tile([P, W], U8, name=name + "_s", tag=name + "_s", align_bytes=64)
+            return c, s
+
+        def quantize(pair, grouped, a=0, b=W):
+            nc.vector.quantize_mx(
+                out=pair[0][:, a:b].bitcast(FP8X4),
+                scales=pair[1][:, a:b],
+                in_=grouped[:, a:b, :].rearrange("p n j -> p (n j)"),
+            )
+
+        def copy_on(eng, out, in_):
+            if eng == "V":
+                nc.vector.tensor_copy(out=out, in_=in_)
+            else:
+                nc.scalar.copy(out=out, in_=in_)
+
+        def interleave(eng, dst, src):
+            copy_on(eng, dst.rearrange("p (c i) j -> p c j i", i=4), src.rearrange("p j (c i) -> p c j i", i=4))
+
+        at_c, wz_c, wm_c, m_c, z_c, mn_c = {}, {}, {}, {}, {}, {}
+        grp, pln, u_sb, accs, xgr = {}, {}, {}, {}, {}
+
+        def wgroup():
+            return work.tile([P, W, PACK], BF16, name="wgrp", tag="wgrp", bufs=4, align_bytes=64)
+
+        def at_il(g, c):
+            grp["at", g, c] = wgroup()
+            nc.vector.tensor_copy(
+                out=grp["at", g, c][:].rearrange("p (t q) j -> p t q j", t=PACK),
+                in_=at_raw[g, c][:].rearrange("p j (q t) -> p t q j", t=PACK),
+            )
+
+        def at_q(g, c):
+            at_c[g, c] = codes_tile("at%d%d" % (g, c))
+            quantize(at_c[g, c], grp["at", g, c])
+
+        def wm_il(g, c):
+            grp["wm", g, c] = wgroup()
+            interleave("S", grp["wm", g, c][:], wm_raw[g, c][:])
+
+        def wm_q(g, c):
+            wm_c[g, c] = codes_tile("wm%d%d" % (g, c))
+            quantize(wm_c[g, c], grp["wm", g, c])
+
+        def wz_w(g, c):
+            planar = work.tile([P, PACK, W], BF16, name="wzp", tag="wzp", bufs=3, align_bytes=64)
+            for t in range(PACK):
+                nc.scalar.activation(
+                    out=planar[:, t, :],
+                    in_=wz_raw[g][:, t, c * W : (c + 1) * W].bitcast(FP8),
+                    func=ACT.Copy,
+                    scale=sc_sb[:, g, t : t + 1],
+                )
+            pln["wz", g, c] = planar
+
+        def wz_il(g, c):
+            grp["wz", g, c] = wgroup()
+            interleave("V", grp["wz", g, c][:], pln["wz", g, c][:])
+
+        def wz_q(g, c):
+            wz_c[g, c] = codes_tile("wz%d%d" % (g, c))
+            quantize(wz_c[g, c], grp["wz", g, c])
+
+        def turn(kind, h, g):
+            rows = m_raw if kind == "m" else z_raw
+            grouped = work.tile([P, W, PACK], BF16, name="xgrp", tag="xgrp", bufs=5, align_bytes=64)
+            words = grouped[:].rearrange("p n j -> p (n j)").bitcast(F32)
+            for b in range(2):
+                xt = psum.tile([P, 2, 2, P], F32, name="xt", tag="xt", bufs=3)
+                for i in range(2):
+                    src = rows[h * 4 + b * 2 + i][:].bitcast(F32)
+                    for u in range(2):
+                        nc.tensor.transpose(xt[:, i, u, :], src[:, 256 * g + u : 256 * (g + 1) : 2], ident[:])
+                nc.scalar.copy(
+                    out=words[:, b * W : (b + 1) * W].rearrange("p (i r u) -> p i r u", i=2, u=2),
+                    in_=xt[:].rearrange("p i u r -> p i r u"),
+                )
+            xgr[kind, h, g] = grouped
+
+        def x_q(kind, h, g):
+            store = m_c if kind == "m" else z_c
+            store[h, g] = codes_tile("%s%d%d" % (kind, h, g))
+            quantize(store[h, g], xgr[kind, h, g])
+
+        def scalar_u(h):
+            acc = psum.tile([P, W], F32, name="acc", tag="acc", bufs=5)
+            for g in range(ZG):
+                for t in range(PACK):
+                    nc.tensor.matmul(
+                        acc[:],
+                        lhsT=ez_sb[:, g, t : t + 1].to_broadcast([P, P]),
+                        rhs=xgr["z", h, g][:, :, t],
+                        start=(g == 0 and t == 0),
+                        stop=(g == ZG - 1 and t == PACK - 1),
+                    )
+            u_sb[h] = keep.tile([P, W], F32, name="u%d" % h, tag="u%d" % h)
+            nc.scalar.copy(out=u_sb[h][:], in_=acc[:])
+
+        def mx(acc, lhs, lcols, rhs, start, stop):
+            nc.tensor.matmul_mx(
+                out=acc[:],
+                lhsT=lhs[0][:, lcols].bitcast(FP8X4),
+                lhsT_scale=lhs[1][:, lcols],
+                rhs=rhs[0][:].bitcast(FP8X4),
+                rhs_scale=rhs[1][:],
+                start=start,
+                stop=stop,
+            )
+
+        def stage1(h, c, t):
+            if t == 0:
+                pln["mn", h, c] = work.tile([P, PACK, W], BF16, name="mnp", tag="mnp", bufs=3, align_bytes=64)
+            acc = psum.tile([P, W], F32, name="acc", tag="acc", bufs=5)
+            for g in range(MG):
+                mx(acc, at_c[g, c], slice(t * P, (t + 1) * P), m_c[h, g], g == 0, g == MG - 1)
+            nc.vector.scalar_tensor_tensor(
+                out=pln["mn", h, c][:, t, :],
+                in0=u_sb[h][:],
+                scalar=bv_sb[:, c, t : t + 1],
+                in1=acc[:],
+                op0=ALU.mult,
+                op1=ALU.add,
+            )
+
+        def mn_il(h, c, s):
+            if s == 0:
+                grp["mn", h, c] = work.tile([P, W, PACK], BF16, name="mngrp", tag="mngrp", bufs=3, align_bytes=64)
+                mn_c[h, c] = codes_tile("mn%d%d" % (h, c))
+            cols = slice(s * 256, s * 256 + 256)
+            interleave("VVSV"[h * 2 + c], grp["mn", h, c][:, cols, :], pln["mn", h, c][:, :, cols])
+
+        def mn_q(h, c, s):
+            quantize(mn_c[h, c], grp["mn", h, c], s * 256, s * 256 + 256)
+
+        def zw(h, i, c):
+            accs[h, i, c] = psum.tile([P, W], F32, name="acc", tag="acc", bufs=5)
+            for g in range(ZG):
+                mx(accs[h, i, c], z_c[h, g], slice(i * P, (i + 1) * P), wz_c[g, c], g == 0, False)
+
+        def mw(h, i, c):
+            acc = accs[h, i, c]
+            for g in range(MG):
+                mx(acc, mn_c[h, g], slice(i * P, (i + 1) * P), wm_c[g, c], False, g == MG - 1)
+            res = work.tile([P, W], F32, name="res", tag="res", bufs=4)
+            nc.scalar.activation(out=res[:], in_=acc[:], func=ACT.Tanh)
+            nc.sync.dma_start(out=out[(h * 4 + i) * P : (h * 4 + i + 1) * P, c * W : (c + 1) * W], in_=res[:])
+
+
+        load_w(at_raw, at_src, 0, 0)
+        load_m(0)
+        load_m(1)
+        load_w(at_raw, at_src, 1, 0)
+        load_m(2)
+        load_m(3)
+        nc.sync.dma_start(out=ez_sb[:], in_=ez.rearrange("(g p j) -> p g j", p=P, j=PACK))
+        nc.sync.dma_start(out=bv_sb[:], in_=bvec.rearrange("(g p j) -> p g j", p=P, j=PACK))
+        nc.sync.dma_start(out=sc_sb[:], in_=wz_scale.rearrange("(g p j) o -> p g (j o)", p=P, j=PACK))
+        for i in range(4):
+            load_z(i)
+        for g in range(MG):
+            load_w(at_raw, at_src, g, 1)
+        for g in range(ZG):
+            load_wz(g)
+        load_m(4)
+        load_m(5)
+
+        for g in range(MG):
+            at_il(g, 0)
+            at_q(g, 0)
+        for g in range(MG):
+            turn("m", 0, g)
+        for g in range(MG):
+            x_q("m", 0, g)
+        load_m(6)
+        load_m(7)
+        for g in range(ZG):
+            turn("z", 0, g)
+        for i in range(4, 7):
+            load_z(i)
+        scalar_u(0)
+        for t in range(PACK):
+            stage1(0, 0, t)
+        for g in range(MG):
+            at_il(g, 1)
+            at_q(g, 1)
+        for t in range(PACK):
+            stage1(0, 1, t)
+        load_z(7)
+        for c in range(2):
+            for g in range(MG):
+                load_w(wm_raw, wm_src, g, c)
+        for g in range(MG):
+            turn("m", 1, g)
+        for g in range(MG):
+            x_q("m", 1, g)
+        for g in range(ZG):
+            x_q("z", 0, g)
+        for g in range(ZG):
+            turn("z", 1, g)
+        scalar_u(1)
+        for c in range(2):
+            for t in range(PACK):
+                stage1(1, c, t)
+        for c in range(2):
+            for g in range(ZG):
+                wz_w(g, c)
+                wz_il(g, c)
+                wz_q(g, c)
+            if c == 0:
+                for g in range(ZG):
+                    x_q("z", 1, g)
+                for h in range(2):
+                    for s in range(2):
+                        for g in range(MG):
+                            mn_il(h, g, s)
+                            mn_q(h, g, s)
+            for g in range(MG):
+                wm_il(g, c)
+                wm_q(g, c)
+            for h in range(2):
+                for i in range(4):
+                    zw(h, i, c)
+                    mw(h, i, c)

@@ -24,6 +24,230 @@ MG = P_MEM // PASS
 HALVES = N // W
 
 
+XT = 3
+ACC = 5
+MGB = 2
+ZPB = 4
+
+
+ORDER = [
+    ("LD", "at", 0, 0),
+    ("LD", "m", 0),
+    ("LD", "m", 1),
+    ("LD", "at", 1, 0),
+    ("LD", "m", 2),
+    ("LD", "m", 3),
+    ("LD", "x"),
+    ("ATI", 0, 0, "V"),
+    ("LD", "z", 0),
+    ("LD", "z", 1),
+    ("T", "m", 0, 0, 0),
+    ("EV", "m", 0, 0, 0),
+    ("T", "m", 0, 1, 0),
+    ("EV", "m", 0, 1, 0),
+    ("LD", "z", 2),
+    ("ATI", 1, 0, "V"),
+    ("LD", "z", 3),
+    ("LD", "at", 0, 1),
+    ("LD", "at", 1, 1),
+    ("LD", "wz", 0),
+    ("T", "m", 0, 0, 1),
+    ("LD", "wz", 1),
+    ("Q", "at", 0, 0),
+    ("EV", "m", 0, 0, 1),
+    ("T", "m", 0, 1, 1),
+    ("LD", "wz", 2),
+    ("Q", "at", 1, 0),
+    ("EV", "m", 0, 1, 1),
+    ("Q", "m", 0, 0),
+    ("LD", "m", 4),
+    ("T", "z", 0, 0, 0),
+    ("Q", "m", 0, 1),
+    ("EV", "z", 0, 0, 0),
+    ("LD", "m", 5),
+    ("LD", "m", 6),
+    ("T", "z", 0, 0, 1),
+    ("EV", "z", 0, 0, 1),
+    ("T", "z", 0, 1, 0),
+    ("EV", "z", 0, 1, 0),
+    ("LD", "m", 7),
+    ("ATI", 0, 1, "V"),
+    ("T", "z", 0, 1, 1),
+    ("EV", "z", 0, 1, 1),
+    ("T", "z", 0, 2, 0),
+    ("LD", "z", 4),
+    ("EV", "z", 0, 2, 0),
+    ("T", "z", 0, 2, 1),
+    ("ZI", 0, 0),
+    ("EV", "z", 0, 2, 1),
+    ("Q", "at", 0, 1),
+    ("LD", "z", 5),
+    ("U", 0, 0),
+    ("ZI", 0, 1),
+    ("Q", "z", 0, 0),
+    ("LD", "z", 6),
+    ("U", 0, 1),
+    ("ATI", 1, 1, "V"),
+    ("WZ", 0, 0),
+    ("U", 0, 2),
+    ("LD", "z", 7),
+    ("UE", 0),
+    ("S1", 0, 0, 0),
+    ("LD", "wm", 0, 0),
+    ("ZI", 0, 2),
+    ("S1", 0, 0, 1),
+    ("LD", "wm", 1, 0),
+    ("Q", "z", 0, 1),
+    ("S1", 0, 0, 2),
+    ("LD", "wm", 0, 1),
+    ("Q", "at", 1, 1),
+    ("S1", 0, 0, 3),
+    ("LD", "wm", 1, 1),
+    ("WZI", 0, 0, "V"),
+    ("WZ", 1, 0),
+    ("T", "m", 1, 0, 0),
+    ("EV", "m", 1, 0, 0),
+    ("T", "m", 1, 1, 0),
+    ("Q", "z", 0, 2),
+    ("EV", "m", 1, 1, 0),
+    ("T", "m", 1, 0, 1),
+    ("STT", 0, 0, 0),
+    ("EV", "m", 1, 0, 1),
+    ("T", "m", 1, 1, 1),
+    ("STT", 0, 0, 1),
+    ("EV", "m", 1, 1, 1),
+    ("S1", 0, 1, 0),
+    ("STT", 0, 0, 2),
+    ("S1", 0, 1, 1),
+    ("STT", 0, 0, 3),
+    ("S1", 0, 1, 2),
+    ("Q", "wz", 0, 0),
+    ("S1", 0, 1, 3),
+    ("WZI", 1, 0, "V"),
+    ("WZ", 2, 0),
+    ("T", "z", 1, 0, 0),
+    ("EV", "z", 1, 0, 0),
+    ("T", "z", 1, 0, 1),
+    ("STT", 0, 1, 0),
+    ("EV", "z", 1, 0, 1),
+    ("T", "z", 1, 1, 0),
+    ("STT", 0, 1, 1),
+    ("EV", "z", 1, 1, 0),
+    ("T", "z", 1, 1, 1),
+    ("STT", 0, 1, 2),
+    ("T", "z", 1, 2, 0),
+    ("EV", "z", 1, 1, 1),
+    ("STT", 0, 1, 3),
+    ("T", "z", 1, 2, 1),
+    ("EV", "z", 1, 2, 0),
+    ("MNI", 0, 0, "V"),
+    ("EV", "z", 1, 2, 1),
+    ("U", 1, 0),
+    ("WMI", 0, 0, "S"),
+    ("Q", "wz", 1, 0),
+    ("WZI", 2, 0, "V"),
+    ("U", 1, 1),
+    ("U", 1, 2),
+    ("Q", "mn", 0, 0),
+    ("UE", 1),
+    ("Q", "m", 1, 0),
+    ("WMI", 1, 0, "S"),
+    ("Q", "m", 1, 1),
+    ("Q", "wz", 2, 0),
+    ("S1", 1, 0, 0),
+    ("MNI", 0, 1, "V"),
+    ("S1", 1, 0, 1),
+    ("S1", 1, 0, 2),
+    ("S1", 1, 0, 3),
+    ("ZI", 1, 0),
+    ("S1", 1, 1, 0),
+    ("ZI", 1, 1),
+    ("Q", "mn", 0, 1),
+    ("WZ", 0, 1),
+    ("Q", "z", 1, 0),
+    ("Q", "z", 1, 1),
+    ("ZI", 1, 2),
+    ("STT", 1, 0, 0),
+    ("WZ", 1, 1),
+    ("STT", 1, 0, 1),
+    ("S1", 1, 1, 1),
+    ("STT", 1, 0, 2),
+    ("S1", 1, 1, 2),
+    ("STT", 1, 0, 3),
+    ("S1", 1, 1, 3),
+    ("Q", "z", 1, 2),
+    ("WZ", 2, 1),
+    ("Q", "wm", 0, 0),
+    ("ZW", 0, 0, 0),
+    ("STT", 1, 1, 0),
+    ("STT", 1, 1, 1),
+    ("STT", 1, 1, 2),
+    ("ZW", 0, 1, 0),
+    ("STT", 1, 1, 3),
+    ("ZW", 0, 2, 0),
+    ("Q", "wm", 1, 0),
+    ("MNI", 1, 1, "S"),
+    ("MNI", 1, 0, "V"),
+    ("ZW", 0, 3, 0),
+    ("MW", 0, 0, 0),
+    ("MW", 0, 1, 0),
+    ("WZI", 0, 1, "V"),
+    ("MW", 0, 2, 0),
+    ("OUT", 0, 0, 0),
+    ("MW", 0, 3, 0),
+    ("OUT", 0, 1, 0),
+    ("Q", "mn", 1, 0),
+    ("OUT", 0, 2, 0),
+    ("WZI", 1, 1, "V"),
+    ("ZW", 1, 0, 0),
+    ("OUT", 0, 3, 0),
+    ("ZW", 1, 1, 0),
+    ("WMI", 0, 1, "S"),
+    ("Q", "mn", 1, 1),
+    ("Q", "wz", 0, 1),
+    ("ZW", 1, 2, 0),
+    ("WZI", 2, 1, "V"),
+    ("ZW", 1, 3, 0),
+    ("MW", 1, 0, 0),
+    ("Q", "wz", 1, 1),
+    ("OUT", 1, 0, 0),
+    ("MW", 1, 1, 0),
+    ("Q", "wm", 0, 1),
+    ("OUT", 1, 1, 0),
+    ("MW", 1, 2, 0),
+    ("WMI", 1, 1, "S"),
+    ("Q", "wz", 2, 1),
+    ("MW", 1, 3, 0),
+    ("ZW", 0, 0, 1),
+    ("ZW", 0, 1, 1),
+    ("OUT", 1, 2, 0),
+    ("Q", "wm", 1, 1),
+    ("ZW", 0, 2, 1),
+    ("OUT", 1, 3, 0),
+    ("ZW", 0, 3, 1),
+    ("MW", 0, 0, 1),
+    ("OUT", 0, 0, 1),
+    ("MW", 0, 1, 1),
+    ("OUT", 0, 1, 1),
+    ("MW", 0, 2, 1),
+    ("MW", 0, 3, 1),
+    ("OUT", 0, 2, 1),
+    ("OUT", 0, 3, 1),
+    ("ZW", 1, 0, 1),
+    ("ZW", 1, 1, 1),
+    ("ZW", 1, 2, 1),
+    ("ZW", 1, 3, 1),
+    ("MW", 1, 0, 1),
+    ("OUT", 1, 0, 1),
+    ("MW", 1, 1, 1),
+    ("OUT", 1, 1, 1),
+    ("MW", 1, 2, 1),
+    ("OUT", 1, 2, 1),
+    ("MW", 1, 3, 1),
+    ("OUT", 1, 3, 1),
+]
+
+
 def tile_legendrememoryunitstep_kernel(tc, z, m, ez, at, bvec, wz_bytes, wz_scale, wm, out):
     nc = tc.nc
     with ExitStack() as ctx:
@@ -87,32 +311,83 @@ def tile_legendrememoryunitstep_kernel(tc, z, m, ez, at, bvec, wz_bytes, wz_scal
         def interleave(eng, dst, src):
             copy_on(eng, dst.rearrange("p (c i) j -> p c j i", i=4), src.rearrange("p j (c i) -> p c j i", i=4))
 
-        at_c, wz_c, wm_c, m_c, z_c, mn_c = {}, {}, {}, {}, {}, {}
-        grp, pln, u_sb, accs, xgr = {}, {}, {}, {}, {}
+        codes, grp, pln, accs, xts, u_sb, tasks = {}, {}, {}, {}, {}, {}, {}
 
-        def wgroup():
-            return work.tile([P, W, PACK], BF16, name="wgrp", tag="wgrp", bufs=4, align_bytes=64)
-
-        def at_il(g, c):
-            grp["at", g, c] = wgroup()
-            nc.vector.tensor_copy(
-                out=grp["at", g, c][:].rearrange("p (t q) j -> p t q j", t=PACK),
-                in_=at_raw[g, c][:].rearrange("p j (q t) -> p t q j", t=PACK),
+        def mx(acc, lhs, lcols, rhs, start, stop):
+            nc.tensor.matmul_mx(
+                out=acc[:],
+                lhsT=codes[lhs][0][:, lcols].bitcast(FP8X4),
+                lhsT_scale=codes[lhs][1][:, lcols],
+                rhs=codes[rhs][0][:].bitcast(FP8X4),
+                rhs_scale=codes[rhs][1][:],
+                start=start,
+                stop=stop,
             )
 
-        def at_q(g, c):
-            at_c[g, c] = codes_tile("at%d%d" % (g, c))
-            quantize(at_c[g, c], grp["at", g, c])
+        def T(kind, h, g, b):
+            rows = m_raw if kind == "m" else z_raw
+            xt = psum.tile([P, 2, 2, P], F32, name="xt", tag="xt", bufs=XT)
+            for i in range(2):
+                src = rows[h * 4 + b * 2 + i][:].bitcast(F32)
+                for u in range(2):
+                    nc.tensor.transpose(xt[:, i, u, :], src[:, 256 * g + u : 256 * (g + 1) : 2], ident[:])
+            xts[kind, h, g, b] = xt
 
-        def wm_il(g, c):
-            grp["wm", g, c] = wgroup()
-            interleave("S", grp["wm", g, c][:], wm_raw[g, c][:])
+        def U(h, g):
+            if g == 0:
+                accs["u", h] = psum.tile([P, W], F32, name="acc", tag="acc", bufs=ACC)
+            for t in range(PACK):
+                nc.tensor.matmul(
+                    accs["u", h][:],
+                    lhsT=ez_sb[:, g, t : t + 1].to_broadcast([P, P]),
+                    rhs=zview(h, g, t),
+                    start=(g == 0 and t == 0),
+                    stop=(g == ZG - 1 and t == PACK - 1),
+                )
 
-        def wm_q(g, c):
-            wm_c[g, c] = codes_tile("wm%d%d" % (g, c))
-            quantize(wm_c[g, c], grp["wm", g, c])
+        def zview(h, g, t):
+            v = pln["z", h, g][:, t // 2, :].bitcast(BF16)
+            return v[:, t % 2 : 2 * W : 2]
 
-        def wz_w(g, c):
+        def S1(h, c, t):
+            acc = psum.tile([P, W], F32, name="acc", tag="acc", bufs=ACC)
+            accs["s", h, c, t] = acc
+            for g in range(MG):
+                mx(acc, ("at", g, c), slice(t * P, (t + 1) * P), ("m", h, g), g == 0, g == MG - 1)
+
+        def ZW(h, i, c):
+            acc = psum.tile([P, W], F32, name="acc", tag="acc", bufs=ACC)
+            accs["o", h, i, c] = acc
+            for g in range(ZG):
+                mx(acc, ("z", h, g), slice(i * P, (i + 1) * P), ("wz", g, c), g == 0, False)
+
+        def MW(h, i, c):
+            for g in range(MG):
+                mx(accs["o", h, i, c], ("mn", h, g), slice(i * P, (i + 1) * P), ("wm", g, c), False, g == MG - 1)
+
+        def EV(kind, h, g, b):
+            xt = xts[kind, h, g, b]
+            if kind == "m":
+                if b == 0:
+                    grp["m", h, g] = work.tile([P, W, PACK], BF16, name="mg", tag="mg", bufs=MGB, align_bytes=64)
+                words = grp["m", h, g][:].rearrange("p n j -> p (n j)").bitcast(F32)
+                nc.scalar.copy(
+                    out=words[:, b * W : (b + 1) * W].rearrange("p (i r u) -> p i r u", i=2, u=2),
+                    in_=xt[:].rearrange("p i u r -> p i r u"),
+                )
+            else:
+                if b == 0:
+                    pln["z", h, g] = work.tile([P, 2, W], F32, name="zp", tag="zp", bufs=ZPB, align_bytes=64)
+                nc.scalar.copy(
+                    out=pln["z", h, g][:, :, b * 256 : (b + 1) * 256].rearrange("p u (i r) -> p u i r", i=2),
+                    in_=xt[:].rearrange("p i u r -> p u i r"),
+                )
+
+        def UE(h):
+            u_sb[h] = keep.tile([P, W], F32, name="u%d" % h, tag="u%d" % h)
+            nc.scalar.copy(out=u_sb[h][:], in_=accs["u", h][:])
+
+        def WZ(g, c):
             planar = work.tile([P, PACK, W], BF16, name="wzp", tag="wzp", bufs=3, align_bytes=64)
             for t in range(PACK):
                 nc.scalar.activation(
@@ -123,171 +398,82 @@ def tile_legendrememoryunitstep_kernel(tc, z, m, ez, at, bvec, wz_bytes, wz_scal
                 )
             pln["wz", g, c] = planar
 
-        def wz_il(g, c):
-            grp["wz", g, c] = wgroup()
-            interleave("V", grp["wz", g, c][:], pln["wz", g, c][:])
+        def OUT(h, i, c):
+            res = work.tile([P, W], F32, name="res", tag="res", bufs=4)
+            nc.scalar.activation(out=res[:], in_=accs["o", h, i, c][:], func=ACT.Tanh)
+            nc.sync.dma_start(out=out[(h * 4 + i) * P : (h * 4 + i + 1) * P, c * W : (c + 1) * W], in_=res[:])
 
-        def wz_q(g, c):
-            wz_c[g, c] = codes_tile("wz%d%d" % (g, c))
-            quantize(wz_c[g, c], grp["wz", g, c])
+        def wgroup(e):
+            tag = "wg" + e
+            return work.tile([P, W, PACK], BF16, name=tag, tag=tag, bufs=3 if e == "V" else 2, align_bytes=64)
 
-        def turn(kind, h, g):
-            rows = m_raw if kind == "m" else z_raw
-            grouped = work.tile([P, W, PACK], BF16, name="xgrp", tag="xgrp", bufs=5, align_bytes=64)
-            words = grouped[:].rearrange("p n j -> p (n j)").bitcast(F32)
-            for b in range(2):
-                xt = psum.tile([P, 2, 2, P], F32, name="xt", tag="xt", bufs=3)
-                for i in range(2):
-                    src = rows[h * 4 + b * 2 + i][:].bitcast(F32)
-                    for u in range(2):
-                        nc.tensor.transpose(xt[:, i, u, :], src[:, 256 * g + u : 256 * (g + 1) : 2], ident[:])
-                nc.scalar.copy(
-                    out=words[:, b * W : (b + 1) * W].rearrange("p (i r u) -> p i r u", i=2, u=2),
-                    in_=xt[:].rearrange("p i u r -> p i r u"),
-                )
-            xgr[kind, h, g] = grouped
-
-        def x_q(kind, h, g):
-            store = m_c if kind == "m" else z_c
-            store[h, g] = codes_tile("%s%d%d" % (kind, h, g))
-            quantize(store[h, g], xgr[kind, h, g])
-
-        def scalar_u(h):
-            acc = psum.tile([P, W], F32, name="acc", tag="acc", bufs=5)
-            for g in range(ZG):
-                for t in range(PACK):
-                    nc.tensor.matmul(
-                        acc[:],
-                        lhsT=ez_sb[:, g, t : t + 1].to_broadcast([P, P]),
-                        rhs=xgr["z", h, g][:, :, t],
-                        start=(g == 0 and t == 0),
-                        stop=(g == ZG - 1 and t == PACK - 1),
-                    )
-            u_sb[h] = keep.tile([P, W], F32, name="u%d" % h, tag="u%d" % h)
-            nc.scalar.copy(out=u_sb[h][:], in_=acc[:])
-
-        def mx(acc, lhs, lcols, rhs, start, stop):
-            nc.tensor.matmul_mx(
-                out=acc[:],
-                lhsT=lhs[0][:, lcols].bitcast(FP8X4),
-                lhsT_scale=lhs[1][:, lcols],
-                rhs=rhs[0][:].bitcast(FP8X4),
-                rhs_scale=rhs[1][:],
-                start=start,
-                stop=stop,
+        def ATI(g, c, e):
+            grp["at", g, c] = wgroup(e)
+            copy_on(
+                e,
+                grp["at", g, c][:].rearrange("p (t q) j -> p t q j", t=PACK),
+                at_raw[g, c][:].rearrange("p j (q t) -> p t q j", t=PACK),
             )
 
-        def stage1(h, c, t):
+        def WMI(g, c, e):
+            grp["wm", g, c] = wgroup(e)
+            interleave(e, grp["wm", g, c][:], wm_raw[g, c][:])
+
+        def WZI(g, c, e):
+            grp["wz", g, c] = wgroup(e)
+            interleave(e, grp["wz", g, c][:], pln["wz", g, c][:])
+
+        def ZI(h, g):
+            grp["z", h, g] = work.tile([P, W, PACK], BF16, name="zg", tag="zg", bufs=2, align_bytes=64)
+            nc.vector.tensor_copy(
+                out=grp["z", h, g][:].rearrange("p n j -> p (n j)").bitcast(F32).rearrange("p (n u) -> p n u", u=2),
+                in_=pln["z", h, g][:].rearrange("p u n -> p n u"),
+            )
+
+        def STT(h, c, t):
             if t == 0:
                 pln["mn", h, c] = work.tile([P, PACK, W], BF16, name="mnp", tag="mnp", bufs=3, align_bytes=64)
-            acc = psum.tile([P, W], F32, name="acc", tag="acc", bufs=5)
-            for g in range(MG):
-                mx(acc, at_c[g, c], slice(t * P, (t + 1) * P), m_c[h, g], g == 0, g == MG - 1)
             nc.vector.scalar_tensor_tensor(
                 out=pln["mn", h, c][:, t, :],
                 in0=u_sb[h][:],
                 scalar=bv_sb[:, c, t : t + 1],
-                in1=acc[:],
+                in1=accs["s", h, c, t][:],
                 op0=ALU.mult,
                 op1=ALU.add,
             )
 
-        def mn_il(h, c, s):
-            if s == 0:
-                grp["mn", h, c] = work.tile([P, W, PACK], BF16, name="mngrp", tag="mngrp", bufs=3, align_bytes=64)
-                mn_c[h, c] = codes_tile("mn%d%d" % (h, c))
-            cols = slice(s * 256, s * 256 + 256)
-            interleave("VVSV"[h * 2 + c], grp["mn", h, c][:, cols, :], pln["mn", h, c][:, :, cols])
+        def MNI(h, c, e):
+            tag = "mng" + e
+            grp["mn", h, c] = work.tile([P, W, PACK], BF16, name=tag, tag=tag, bufs=2, align_bytes=64)
+            interleave(e, grp["mn", h, c][:], pln["mn", h, c][:])
 
-        def mn_q(h, c, s):
-            quantize(mn_c[h, c], grp["mn", h, c], s * 256, s * 256 + 256)
+        def Q(*key):
+            name = "".join(str(k) for k in (("m",) + key[1:] if key[0] == "mn" else key))
+            codes[key] = codes_tile(name)
+            quantize(codes[key], grp[key])
+        def dispatch(key):
+            kind = key[0]
+            if kind == "LD":
+                if key[1] == "at":
+                    load_w(at_raw, at_src, key[2], key[3])
+                elif key[1] == "wm":
+                    load_w(wm_raw, wm_src, key[2], key[3])
+                elif key[1] == "m":
+                    load_m(key[2])
+                elif key[1] == "z":
+                    load_z(key[2])
+                elif key[1] == "wz":
+                    load_wz(key[2])
+                else:
+                    nc.sync.dma_start(out=ez_sb[:], in_=ez.rearrange("(g p j) -> p g j", p=P, j=PACK))
+                    nc.sync.dma_start(out=bv_sb[:], in_=bvec.rearrange("(g p j) -> p g j", p=P, j=PACK))
+                    nc.sync.dma_start(out=sc_sb[:], in_=wz_scale.rearrange("(g p j) o -> p g (j o)", p=P, j=PACK))
+            else:
+                FN[kind](*key[1:])
 
-        def zw(h, i, c):
-            accs[h, i, c] = psum.tile([P, W], F32, name="acc", tag="acc", bufs=5)
-            for g in range(ZG):
-                mx(accs[h, i, c], z_c[h, g], slice(i * P, (i + 1) * P), wz_c[g, c], g == 0, False)
+        FN = {"T": T, "U": U, "S1": S1, "ZW": ZW, "MW": MW, "EV": EV, "UE": UE, "WZ": WZ, "OUT": OUT, "ATI": ATI,
+              "WMI": WMI, "WZI": WZI, "ZI": ZI, "STT": STT, "MNI": MNI, "Q": Q}
 
-        def mw(h, i, c):
-            acc = accs[h, i, c]
-            for g in range(MG):
-                mx(acc, mn_c[h, g], slice(i * P, (i + 1) * P), wm_c[g, c], False, g == MG - 1)
-            res = work.tile([P, W], F32, name="res", tag="res", bufs=4)
-            nc.scalar.activation(out=res[:], in_=acc[:], func=ACT.Tanh)
-            nc.sync.dma_start(out=out[(h * 4 + i) * P : (h * 4 + i + 1) * P, c * W : (c + 1) * W], in_=res[:])
-
-
-        load_w(at_raw, at_src, 0, 0)
-        load_m(0)
-        load_m(1)
-        load_w(at_raw, at_src, 1, 0)
-        load_m(2)
-        load_m(3)
-        nc.sync.dma_start(out=ez_sb[:], in_=ez.rearrange("(g p j) -> p g j", p=P, j=PACK))
-        nc.sync.dma_start(out=bv_sb[:], in_=bvec.rearrange("(g p j) -> p g j", p=P, j=PACK))
-        nc.sync.dma_start(out=sc_sb[:], in_=wz_scale.rearrange("(g p j) o -> p g (j o)", p=P, j=PACK))
-        for i in range(4):
-            load_z(i)
-        for g in range(MG):
-            load_w(at_raw, at_src, g, 1)
-        for g in range(ZG):
-            load_wz(g)
-        load_m(4)
-        load_m(5)
-
-        for g in range(MG):
-            at_il(g, 0)
-            at_q(g, 0)
-        for g in range(MG):
-            turn("m", 0, g)
-        for g in range(MG):
-            x_q("m", 0, g)
-        load_m(6)
-        load_m(7)
-        for g in range(ZG):
-            turn("z", 0, g)
-        for i in range(4, 7):
-            load_z(i)
-        scalar_u(0)
-        for t in range(PACK):
-            stage1(0, 0, t)
-        for g in range(MG):
-            at_il(g, 1)
-            at_q(g, 1)
-        for t in range(PACK):
-            stage1(0, 1, t)
-        load_z(7)
-        for c in range(2):
-            for g in range(MG):
-                load_w(wm_raw, wm_src, g, c)
-        for g in range(MG):
-            turn("m", 1, g)
-        for g in range(MG):
-            x_q("m", 1, g)
-        for g in range(ZG):
-            x_q("z", 0, g)
-        for g in range(ZG):
-            turn("z", 1, g)
-        scalar_u(1)
-        for c in range(2):
-            for t in range(PACK):
-                stage1(1, c, t)
-        for c in range(2):
-            for g in range(ZG):
-                wz_w(g, c)
-                wz_il(g, c)
-                wz_q(g, c)
-            if c == 0:
-                for g in range(ZG):
-                    x_q("z", 1, g)
-                for h in range(2):
-                    for s in range(2):
-                        for g in range(MG):
-                            mn_il(h, g, s)
-                            mn_q(h, g, s)
-            for g in range(MG):
-                wm_il(g, c)
-                wm_q(g, c)
-            for h in range(2):
-                for i in range(4):
-                    zw(h, i, c)
-                    mw(h, i, c)
+        with tc.manual_schedule():
+            for key in ORDER:
+                dispatch(key)

@@ -3,8 +3,8 @@ from contextlib import ExitStack
 import concourse.mybir as mybir
 from concourse.masks import make_identity
 
-N, K, P_MEM, H = 1024, 1536, 1024, 1024
-FLOPS = 2 * N * (K * H + P_MEM * P_MEM + P_MEM * H) + 2 * N * K + 3 * N * P_MEM
+N, K, MEM, H = 1024, 1536, 1024, 1024
+FLOPS = 2 * N * (K * H + MEM * MEM + MEM * H) + 2 * N * K + 3 * N * MEM
 
 F32 = mybir.dt.float32
 BF16 = mybir.dt.bfloat16
@@ -19,461 +19,510 @@ P = 128
 PACK = 4
 PASS = P * PACK
 W = 512
-ZG = K // PASS
-MG = P_MEM // PASS
-HALVES = N // W
+Z_PASSES = K // PASS
+M_PASSES = MEM // PASS
+HALVES = 2
 
-
-XT = 3
-ACC = 5
-MGB = 2
-ZPB = 4
-
-
-ORDER = [
-    ("LD", "at", 0, 0),
-    ("LD", "m", 0),
-    ("LD", "m", 1),
-    ("LD", "at", 1, 0),
-    ("LD", "m", 2),
-    ("LD", "m", 3),
-    ("LD", "x"),
-    ("ATI", 0, 0, "V"),
-    ("LD", "z", 0),
-    ("LD", "z", 1),
-    ("T", "m", 0, 0, 0),
-    ("EV", "m", 0, 0, 0),
-    ("T", "m", 0, 1, 0),
-    ("EV", "m", 0, 1, 0),
-    ("LD", "z", 2),
-    ("ATI", 1, 0, "V"),
-    ("LD", "z", 3),
-    ("LD", "at", 0, 1),
-    ("LD", "at", 1, 1),
-    ("LD", "wz", 0),
-    ("T", "m", 0, 0, 1),
-    ("LD", "wz", 1),
-    ("Q", "at", 0, 0),
-    ("EV", "m", 0, 0, 1),
-    ("T", "m", 0, 1, 1),
-    ("LD", "wz", 2),
-    ("Q", "at", 1, 0),
-    ("EV", "m", 0, 1, 1),
-    ("Q", "m", 0, 0),
-    ("LD", "m", 4),
-    ("T", "z", 0, 0, 0),
-    ("Q", "m", 0, 1),
-    ("EV", "z", 0, 0, 0),
-    ("LD", "m", 5),
-    ("LD", "m", 6),
-    ("T", "z", 0, 0, 1),
-    ("EV", "z", 0, 0, 1),
-    ("T", "z", 0, 1, 0),
-    ("EV", "z", 0, 1, 0),
-    ("LD", "m", 7),
-    ("ATI", 0, 1, "V"),
-    ("T", "z", 0, 1, 1),
-    ("EV", "z", 0, 1, 1),
-    ("T", "z", 0, 2, 0),
-    ("LD", "z", 4),
-    ("EV", "z", 0, 2, 0),
-    ("T", "z", 0, 2, 1),
-    ("ZI", 0, 0),
-    ("EV", "z", 0, 2, 1),
-    ("Q", "at", 0, 1),
-    ("LD", "z", 5),
-    ("U", 0, 0),
-    ("ZI", 0, 1),
-    ("Q", "z", 0, 0),
-    ("LD", "z", 6),
-    ("U", 0, 1),
-    ("ATI", 1, 1, "V"),
-    ("WZ", 0, 0),
-    ("U", 0, 2),
-    ("LD", "z", 7),
-    ("UE", 0),
-    ("S1", 0, 0, 0),
-    ("LD", "wm", 0, 0),
-    ("ZI", 0, 2),
-    ("S1", 0, 0, 1),
-    ("LD", "wm", 1, 0),
-    ("Q", "z", 0, 1),
-    ("S1", 0, 0, 2),
-    ("LD", "wm", 0, 1),
-    ("Q", "at", 1, 1),
-    ("S1", 0, 0, 3),
-    ("LD", "wm", 1, 1),
-    ("WZI", 0, 0, "V"),
-    ("WZ", 1, 0),
-    ("T", "m", 1, 0, 0),
-    ("EV", "m", 1, 0, 0),
-    ("T", "m", 1, 1, 0),
-    ("Q", "z", 0, 2),
-    ("EV", "m", 1, 1, 0),
-    ("T", "m", 1, 0, 1),
-    ("STT", 0, 0, 0),
-    ("EV", "m", 1, 0, 1),
-    ("T", "m", 1, 1, 1),
-    ("STT", 0, 0, 1),
-    ("EV", "m", 1, 1, 1),
-    ("S1", 0, 1, 0),
-    ("STT", 0, 0, 2),
-    ("S1", 0, 1, 1),
-    ("STT", 0, 0, 3),
-    ("S1", 0, 1, 2),
-    ("Q", "wz", 0, 0),
-    ("S1", 0, 1, 3),
-    ("WZI", 1, 0, "V"),
-    ("WZ", 2, 0),
-    ("T", "z", 1, 0, 0),
-    ("EV", "z", 1, 0, 0),
-    ("T", "z", 1, 0, 1),
-    ("STT", 0, 1, 0),
-    ("EV", "z", 1, 0, 1),
-    ("T", "z", 1, 1, 0),
-    ("STT", 0, 1, 1),
-    ("EV", "z", 1, 1, 0),
-    ("T", "z", 1, 1, 1),
-    ("STT", 0, 1, 2),
-    ("T", "z", 1, 2, 0),
-    ("EV", "z", 1, 1, 1),
-    ("STT", 0, 1, 3),
-    ("T", "z", 1, 2, 1),
-    ("EV", "z", 1, 2, 0),
-    ("MNI", 0, 0, "V"),
-    ("EV", "z", 1, 2, 1),
-    ("U", 1, 0),
-    ("WMI", 0, 0, "S"),
-    ("Q", "wz", 1, 0),
-    ("WZI", 2, 0, "V"),
-    ("U", 1, 1),
-    ("U", 1, 2),
-    ("Q", "mn", 0, 0),
-    ("UE", 1),
-    ("Q", "m", 1, 0),
-    ("WMI", 1, 0, "S"),
-    ("Q", "m", 1, 1),
-    ("Q", "wz", 2, 0),
-    ("S1", 1, 0, 0),
-    ("MNI", 0, 1, "V"),
-    ("S1", 1, 0, 1),
-    ("S1", 1, 0, 2),
-    ("S1", 1, 0, 3),
-    ("ZI", 1, 0),
-    ("S1", 1, 1, 0),
-    ("ZI", 1, 1),
-    ("Q", "mn", 0, 1),
-    ("WZ", 0, 1),
-    ("Q", "z", 1, 0),
-    ("Q", "z", 1, 1),
-    ("ZI", 1, 2),
-    ("STT", 1, 0, 0),
-    ("WZ", 1, 1),
-    ("STT", 1, 0, 1),
-    ("S1", 1, 1, 1),
-    ("STT", 1, 0, 2),
-    ("S1", 1, 1, 2),
-    ("STT", 1, 0, 3),
-    ("S1", 1, 1, 3),
-    ("Q", "z", 1, 2),
-    ("WZ", 2, 1),
-    ("Q", "wm", 0, 0),
-    ("ZW", 0, 0, 0),
-    ("STT", 1, 1, 0),
-    ("STT", 1, 1, 1),
-    ("STT", 1, 1, 2),
-    ("ZW", 0, 1, 0),
-    ("STT", 1, 1, 3),
-    ("ZW", 0, 2, 0),
-    ("Q", "wm", 1, 0),
-    ("MNI", 1, 1, "S"),
-    ("MNI", 1, 0, "V"),
-    ("ZW", 0, 3, 0),
-    ("MW", 0, 0, 0),
-    ("MW", 0, 1, 0),
-    ("WZI", 0, 1, "V"),
-    ("MW", 0, 2, 0),
-    ("OUT", 0, 0, 0),
-    ("MW", 0, 3, 0),
-    ("OUT", 0, 1, 0),
-    ("Q", "mn", 1, 0),
-    ("OUT", 0, 2, 0),
-    ("WZI", 1, 1, "V"),
-    ("ZW", 1, 0, 0),
-    ("OUT", 0, 3, 0),
-    ("ZW", 1, 1, 0),
-    ("WMI", 0, 1, "S"),
-    ("Q", "mn", 1, 1),
-    ("Q", "wz", 0, 1),
-    ("ZW", 1, 2, 0),
-    ("WZI", 2, 1, "V"),
-    ("ZW", 1, 3, 0),
-    ("MW", 1, 0, 0),
-    ("Q", "wz", 1, 1),
-    ("OUT", 1, 0, 0),
-    ("MW", 1, 1, 0),
-    ("Q", "wm", 0, 1),
-    ("OUT", 1, 1, 0),
-    ("MW", 1, 2, 0),
-    ("WMI", 1, 1, "S"),
-    ("Q", "wz", 2, 1),
-    ("MW", 1, 3, 0),
-    ("ZW", 0, 0, 1),
-    ("ZW", 0, 1, 1),
-    ("OUT", 1, 2, 0),
-    ("Q", "wm", 1, 1),
-    ("ZW", 0, 2, 1),
-    ("OUT", 1, 3, 0),
-    ("ZW", 0, 3, 1),
-    ("MW", 0, 0, 1),
-    ("OUT", 0, 0, 1),
-    ("MW", 0, 1, 1),
-    ("OUT", 0, 1, 1),
-    ("MW", 0, 2, 1),
-    ("MW", 0, 3, 1),
-    ("OUT", 0, 2, 1),
-    ("OUT", 0, 3, 1),
-    ("ZW", 1, 0, 1),
-    ("ZW", 1, 1, 1),
-    ("ZW", 1, 2, 1),
-    ("ZW", 1, 3, 1),
-    ("MW", 1, 0, 1),
-    ("OUT", 1, 0, 1),
-    ("MW", 1, 1, 1),
-    ("OUT", 1, 1, 1),
-    ("MW", 1, 2, 1),
-    ("OUT", 1, 2, 1),
-    ("MW", 1, 3, 1),
-    ("OUT", 1, 3, 1),
-]
+TURN_BANKS = 3
+SUM_BANKS = 5
+GROUPED_V = 6
+GROUPED_S = 5
 
 
 def tile_legendrememoryunitstep_kernel(tc, z, m, ez, at, bvec, wz_bytes, wz_scale, wm, out):
     nc = tc.nc
     with ExitStack() as ctx:
         keep = ctx.enter_context(tc.tile_pool(name="keep", bufs=1))
-        raw = ctx.enter_context(tc.tile_pool(name="raw", bufs=1))
         work = ctx.enter_context(tc.tile_pool(name="work", bufs=1))
         psum = ctx.enter_context(tc.psum_pool(name="psum", bufs=1))
-        at_raw, m_raw, z_raw, wz_raw, wm_raw = {}, {}, {}, {}, {}
-        at_src = at.rearrange("(g p j) w -> g p j w", p=P, j=PACK)
-        wm_src = wm.rearrange("(g p j) w -> g p j w", p=P, j=PACK)
+
+        row_src = {
+            "m": m.rearrange("(h p i) k -> h p i k", h=HALVES, p=P),
+            "z": z.rearrange("(h p i) k -> h p i k", h=HALVES, p=P),
+        }
+        out_dst = out.rearrange("(h p i) k -> h i p k", h=HALVES, p=P)
+        weight_src = {
+            "at": at.rearrange("(g p j) w -> g p j w", p=P, j=PACK),
+            "wm": wm.rearrange("(g p j) w -> g p j w", p=P, j=PACK),
+        }
         wz_src = wz_bytes.rearrange("(g p j) w -> g p j w", p=P, j=PACK)
 
-        def load_w(store, src, g, c):
-            t = raw.tile([P, PACK, W], BF16, name="w_raw", tag="w_raw", bufs=6)
-            nc.sync.dma_start(out=t[:], in_=src[g][:, :, c * W : (c + 1) * W])
-            store[g, c] = t
-
-        def load_m(i):
-            t = raw.tile([P, P_MEM], BF16, name="m_raw", tag="m_raw", bufs=6)
-            nc.sync.dma_start(out=t[:], in_=m[i * P : (i + 1) * P, :])
-            m_raw[i] = t
-
-        def load_z(i):
-            t = raw.tile([P, K], BF16, name="z_raw", tag="z_raw", bufs=7)
-            nc.sync.dma_start(out=t[:], in_=z[i * P : (i + 1) * P, :])
-            z_raw[i] = t
-
-        def load_wz(g):
-            t = raw.tile([P, PACK, H], U8, name="wz_codes_in", tag="wz_codes_in", bufs=3)
-            nc.sync.dma_start(out=t[:], in_=wz_src[g])
-            wz_raw[g] = t
-
-        warm = keep.tile([P, 1], F32, name="warm")
-        nc.vector.memset(warm[:], 0.0)
-        warm_out = keep.tile([P, 1], F32, name="warm_out")
-        nc.scalar.activation(out=warm_out[:], in_=warm[:], func=ACT.Tanh)
+        spark = keep.tile([P, 2], F32, name="spark")
+        nc.vector.memset(spark[:], 0.0)
+        nc.scalar.activation(out=spark[:, 1:2], in_=spark[:, 0:1], func=ACT.Tanh)
         ident = keep.tile([P, P], F32, name="ident")
         make_identity(nc, ident[:])
-        ez_sb = keep.tile([P, ZG, PACK], BF16, name="ez_sb")
-        bv_sb = keep.tile([P, MG, PACK], BF16, name="bv_sb")
-        sc_sb = keep.tile([P, ZG, PACK], F32, name="sc_sb")
+        zeros = keep.tile([P, P], BF16, name="zeros")
+        nc.vector.memset(zeros[:], 0.0)
+        ez_sb = keep.tile([P, Z_PASSES, PACK], BF16, name="ez_sb")
+        bvec_sb = keep.tile([P, M_PASSES, PACK], BF16, name="bvec_sb")
+        scale_sb = keep.tile([P, Z_PASSES, PACK], F32, name="scale_sb")
 
-        def codes_tile(name):
-            c = keep.tile([P, W], U32, name=name, tag=name, align_bytes=64)
-            s = keep.tile([P, W], U8, name=name + "_s", tag=name + "_s", align_bytes=64)
-            return c, s
+        queues = {"sync": [], "tensor": [], "scalar": [], "vector": []}
+        rings = {}
+        raw, turned, words, planar, grouped, codes, sums, u_sb = {}, {}, {}, {}, {}, {}, {}, {}
 
-        def quantize(pair, grouped, a=0, b=W):
-            nc.vector.quantize_mx(
-                out=pair[0][:, a:b].bitcast(FP8X4),
-                scales=pair[1][:, a:b],
-                in_=grouped[:, a:b, :].rearrange("p n j -> p (n j)"),
-            )
+        def task(queue, key, needs, emit):
+            queues[queue].append((key, needs, emit))
 
-        def copy_on(eng, out, in_):
-            if eng == "V":
-                nc.vector.tensor_copy(out=out, in_=in_)
+        def buffer(ring, bufs, last_readers):
+            uses = rings.setdefault(ring, [])
+            uses.append(last_readers)
+            return uses[-1 - bufs] if len(uses) > bufs else []
+
+        def engine_of(queue):
+            return nc.vector.tensor_copy if queue == "vector" else nc.scalar.copy
+
+
+        def load_rows(kind, h, b):
+            def emit():
+                tag = kind + "_raw"
+                t = work.tile([P, 2, MEM if kind == "m" else K], BF16, name=tag, tag=tag, bufs=3)
+                nc.sync.dma_start(out=t[:], in_=row_src[kind][h][:, 2 * b : 2 * b + 2, :])
+                for i in range(2):
+                    raw[kind, h, 2 * b + i] = t[:, i, :]
+
+            last_pass = (M_PASSES if kind == "m" else Z_PASSES) - 1
+            task("sync", ("load", kind, h, b), buffer(kind + "_raw", 3, [("turn", kind, h, last_pass, b)]), emit)
+
+        def load_weight(kind, g):
+            def emit():
+                raw[kind, g] = work.tile([P, PACK, H], BF16, name="w_raw", tag="w_raw", bufs=3)
+                nc.sync.dma_start(out=raw[kind, g][:], in_=weight_src[kind][g])
+
+            readers = [("interleave", kind, g, c) for c in range(HALVES)]
+            task("sync", ("load", kind, g), buffer("w_raw", 3, readers), emit)
+
+        def load_wz(g):
+            def emit():
+                raw["wz", g] = work.tile([P, PACK, H], U8, name="wz_raw", tag="wz_raw", bufs=Z_PASSES)
+                nc.sync.dma_start(out=raw["wz", g][:], in_=wz_src[g])
+
+            task("sync", ("load", "wz", g), [], emit)
+
+        def load_vectors():
+            def emit():
+                nc.sync.dma_start(out=ez_sb[:], in_=ez.rearrange("(g p j) -> p g j", p=P, j=PACK))
+                nc.sync.dma_start(out=bvec_sb[:], in_=bvec.rearrange("(g p j) -> p g j", p=P, j=PACK))
+                nc.sync.dma_start(out=scale_sb[:], in_=wz_scale.rearrange("(g p j) o -> p g (j o)", p=P, j=PACK))
+
+            task("sync", ("load", "vectors"), [], emit)
+
+
+        def turn(kind, h, g, b):
+            def emit():
+                bank = psum.tile([P, 2, 2, P], F32, name="turned", tag="turned", bufs=TURN_BANKS)
+                for i in range(2):
+                    src = raw[kind, h, 2 * b + i].bitcast(F32)
+                    for u in range(2):
+                        nc.tensor.transpose(
+                            bank[:, i, u, :], src[:, 256 * g + u : 256 * (g + 1) : 2], ident[:]
+                        )
+                turned[kind, h, g, b] = bank
+
+            free = buffer("turned", TURN_BANKS, [("empty", kind, h, g, b)])
+            task("tensor", ("turn", kind, h, g, b), [("load", kind, h, b)] + free, emit)
+
+        def empty(kind, h, g, b):
+            def emit():
+                src = turned[kind, h, g, b][:]
+                if kind == "m":
+                    if b == 0:
+                        grouped["m", h, g] = work.tile(
+                            [P, W, PACK], BF16, name="grouped_s", tag="grouped_s", bufs=GROUPED_S, align_bytes=64
+                        )
+                    dst = grouped["m", h, g][:].rearrange("p n j -> p (n j)").bitcast(F32)
+                    nc.scalar.copy(
+                        out=dst[:, b * W : (b + 1) * W].rearrange("p (i r u) -> p i r u", i=2, u=2),
+                        in_=src.rearrange("p i u r -> p i r u"),
+                    )
+                else:
+                    if b == 0:
+                        words[h, g] = work.tile([P, 2, W], F32, name="z_words", tag="z_words", bufs=4)
+                    nc.scalar.copy(
+                        out=words[h, g][:, :, b * 256 : (b + 1) * 256].rearrange("p u (i r) -> p u i r", i=2),
+                        in_=src.rearrange("p i u r -> p u i r"),
+                    )
+
+            free = []
+            if b == 0 and kind == "m":
+                free = buffer("grouped_s", GROUPED_S, [("quantise", "m", h, g)])
+            elif b == 0:
+                free = buffer("z_words", 4, [("group", h, g), ("dot", h, g)])
+            task("scalar", ("empty", kind, h, g, b), [("turn", kind, h, g, b)] + free, emit)
+
+        def group(h, g):
+            def emit():
+                t = work.tile([P, W, PACK], BF16, name="grouped_v", tag="grouped_v", bufs=GROUPED_V, align_bytes=64)
+                nc.vector.tensor_copy(
+                    out=t[:].rearrange("p n j -> p (n j)").bitcast(F32).rearrange("p (n u) -> p n u", u=2),
+                    in_=words[h, g][:].rearrange("p u n -> p n u"),
+                )
+                grouped["z", h, g] = t
+
+            free = buffer("grouped_v", GROUPED_V, [("quantise", "z", h, g)])
+            task("vector", ("group", h, g), [("empty", "z", h, g, b) for b in range(2)] + free, emit)
+
+
+        def dot(h, g):
+            def emit():
+                if g == 0:
+                    sums["u", h] = psum.tile([P, W], F32, name="sums", tag="sums", bufs=SUM_BANKS)
+                for t in range(PACK):
+                    nc.tensor.matmul(
+                        sums["u", h][:],
+                        lhsT=ez_sb[:, g, t : t + 1].to_broadcast([P, P]),
+                        rhs=words[h, g][:, t // 2, :].bitcast(BF16)[:, t % 2 : 2 * W : 2],
+                        start=(g == 0 and t == 0),
+                        stop=(g == Z_PASSES - 1 and t == PACK - 1),
+                    )
+
+            free = buffer("sums", SUM_BANKS, [("keep_u", h)]) if g == 0 else [("dot", h, g - 1)]
+            needs = [("load", "vectors")] + [("empty", "z", h, g, b) for b in range(2)]
+            task("tensor", ("dot", h, g), needs + free, emit)
+
+        def keep_u(h):
+            def emit():
+                u_sb[h] = keep.tile([P, W], F32, name="u%d" % h)
+                nc.scalar.copy(out=u_sb[h][:], in_=sums["u", h][:])
+
+            task("scalar", ("keep_u", h), [("dot", h, Z_PASSES - 1)], emit)
+
+
+        def interleave(queue, kind, a, b):
+            def emit():
+                tag = "grouped_" + queue[0]
+                bufs = GROUPED_V if queue == "vector" else GROUPED_S
+                dst = work.tile([P, W, PACK], BF16, name=tag, tag=tag, bufs=bufs, align_bytes=64)
+                copy = engine_of(queue)
+                if kind == "at":
+                    src = raw["at", a][:, :, b * W : (b + 1) * W]
+                    for t in range(PACK):
+                        copy(
+                            out=dst[:, t * P : (t + 1) * P, :].rearrange("p (c i) j -> p c j i", i=4),
+                            in_=src[:, :, t : W : PACK].rearrange("p j (c i) -> p c j i", i=4),
+                        )
+                else:
+                    src = raw["wm", a][:, :, b * W : (b + 1) * W] if kind == "wm" else planar[kind, a, b][:]
+                    copy(
+                        out=dst[:].rearrange("p (c i) j -> p c j i", i=4),
+                        in_=src.rearrange("p j (c i) -> p c j i", i=4),
+                    )
+                grouped[kind, a, b] = dst
+
+            if kind == "mn":
+                needs = [("add", a, b, PACK - 1)]
+            elif kind == "wz":
+                needs = [("widen", a, b)]
             else:
-                nc.scalar.copy(out=out, in_=in_)
+                needs = [("load", kind, a)]
+            tag = "grouped_" + queue[0]
+            free = buffer(tag, GROUPED_V if queue == "vector" else GROUPED_S, [("quantise", kind, a, b)])
+            task(queue, ("interleave", kind, a, b), needs + free, emit)
 
-        def interleave(eng, dst, src):
-            copy_on(eng, dst.rearrange("p (c i) j -> p c j i", i=4), src.rearrange("p j (c i) -> p c j i", i=4))
+        def widen(g, c):
+            def emit():
+                t = work.tile([P, PACK, W], BF16, name="wz_planar", tag="wz_planar", bufs=3)
+                for j in range(PACK):
+                    nc.scalar.activation(
+                        out=t[:, j, :],
+                        in_=raw["wz", g][:, j, c * W : (c + 1) * W].bitcast(FP8),
+                        func=ACT.Copy,
+                        scale=scale_sb[:, g, j : j + 1],
+                    )
+                planar["wz", g, c] = t
 
-        codes, grp, pln, accs, xts, u_sb, tasks = {}, {}, {}, {}, {}, {}, {}
+            free = buffer("wz_planar", 3, [("interleave", "wz", g, c)])
+            task("scalar", ("widen", g, c), [("load", "wz", g), ("load", "vectors")] + free, emit)
 
-        def mx(acc, lhs, lcols, rhs, start, stop):
+        def quantise(kind, a, b):
+            def emit():
+                name = "%s%d%d" % (kind, a, b)
+                word = keep.tile([P, W], U32, name=name + "_codes", align_bytes=64)
+                scale = keep.tile([P, W], U8, name=name + "_scales", align_bytes=64)
+                nc.vector.quantize_mx(
+                    out=word[:].bitcast(FP8X4),
+                    scales=scale[:],
+                    in_=grouped[kind, a, b][:].rearrange("p n j -> p (n j)"),
+                )
+                codes[kind, a, b] = (word, scale)
+
+            if kind == "m":
+                needs = [("empty", "m", a, b, 1)]
+            elif kind == "z":
+                needs = [("group", a, b)]
+            else:
+                needs = [("interleave", kind, a, b)]
+            task("vector", ("quantise", kind, a, b), needs, emit)
+
+
+        def mx(acc, lhs, columns, rhs, start, stop):
             nc.tensor.matmul_mx(
                 out=acc[:],
-                lhsT=codes[lhs][0][:, lcols].bitcast(FP8X4),
-                lhsT_scale=codes[lhs][1][:, lcols],
+                lhsT=codes[lhs][0][:, columns].bitcast(FP8X4),
+                lhsT_scale=codes[lhs][1][:, columns],
                 rhs=codes[rhs][0][:].bitcast(FP8X4),
                 rhs_scale=codes[rhs][1][:],
                 start=start,
                 stop=stop,
             )
 
-        def T(kind, h, g, b):
-            rows = m_raw if kind == "m" else z_raw
-            xt = psum.tile([P, 2, 2, P], F32, name="xt", tag="xt", bufs=XT)
-            for i in range(2):
-                src = rows[h * 4 + b * 2 + i][:].bitcast(F32)
-                for u in range(2):
-                    nc.tensor.transpose(xt[:, i, u, :], src[:, 256 * g + u : 256 * (g + 1) : 2], ident[:])
-            xts[kind, h, g, b] = xt
+        def step(h, c, t):
+            def emit():
+                sums["mn", h, c, t] = psum.tile([P, W], F32, name="sums", tag="sums", bufs=SUM_BANKS)
+                for g in range(M_PASSES):
+                    columns = slice(t * P, (t + 1) * P)
+                    mx(sums["mn", h, c, t], ("at", g, c), columns, ("m", h, g), g == 0, g == M_PASSES - 1)
 
-        def U(h, g):
-            if g == 0:
-                accs["u", h] = psum.tile([P, W], F32, name="acc", tag="acc", bufs=ACC)
-            for t in range(PACK):
-                nc.tensor.matmul(
-                    accs["u", h][:],
-                    lhsT=ez_sb[:, g, t : t + 1].to_broadcast([P, P]),
-                    rhs=zview(h, g, t),
-                    start=(g == 0 and t == 0),
-                    stop=(g == ZG - 1 and t == PACK - 1),
+            needs = [("quantise", "at", g, c) for g in range(M_PASSES)]
+            needs += [("quantise", "m", h, g) for g in range(M_PASSES)]
+            task("tensor", ("step", h, c, t), needs + buffer("sums", SUM_BANKS, [("add", h, c, t)]), emit)
+
+        def add(h, c, t):
+            def emit():
+                if t == 0:
+                    planar["mn", h, c] = work.tile([P, PACK, W], BF16, name="mn_planar", tag="mn_planar", bufs=3)
+                nc.vector.scalar_tensor_tensor(
+                    out=planar["mn", h, c][:, t, :],
+                    in0=u_sb[h][:],
+                    scalar=bvec_sb[:, c, t : t + 1],
+                    in1=sums["mn", h, c, t][:],
+                    op0=ALU.mult,
+                    op1=ALU.add,
                 )
 
-        def zview(h, g, t):
-            v = pln["z", h, g][:, t // 2, :].bitcast(BF16)
-            return v[:, t % 2 : 2 * W : 2]
+            free = buffer("mn_planar", 3, [("interleave", "mn", h, c)]) if t == 0 else []
+            task("vector", ("add", h, c, t), [("step", h, c, t), ("keep_u", h)] + free, emit)
 
-        def S1(h, c, t):
-            acc = psum.tile([P, W], F32, name="acc", tag="acc", bufs=ACC)
-            accs["s", h, c, t] = acc
-            for g in range(MG):
-                mx(acc, ("at", g, c), slice(t * P, (t + 1) * P), ("m", h, g), g == 0, g == MG - 1)
+        def z_part(h, c, i):
+            def emit():
+                sums["out", h, c, i] = psum.tile([P, W], F32, name="sums", tag="sums", bufs=SUM_BANKS)
+                for g in range(Z_PASSES):
+                    columns = slice(i * P, (i + 1) * P)
+                    mx(sums["out", h, c, i], ("z", h, g), columns, ("wz", g, c), g == 0, False)
 
-        def ZW(h, i, c):
-            acc = psum.tile([P, W], F32, name="acc", tag="acc", bufs=ACC)
-            accs["o", h, i, c] = acc
-            for g in range(ZG):
-                mx(acc, ("z", h, g), slice(i * P, (i + 1) * P), ("wz", g, c), g == 0, False)
+            needs = [("quantise", "z", h, g) for g in range(Z_PASSES)]
+            needs += [("quantise", "wz", g, c) for g in range(Z_PASSES)]
+            task("tensor", ("z_part", h, c, i), needs + buffer("sums", SUM_BANKS, [("finish", h, c, i)]), emit)
 
-        def MW(h, i, c):
-            for g in range(MG):
-                mx(accs["o", h, i, c], ("mn", h, g), slice(i * P, (i + 1) * P), ("wm", g, c), False, g == MG - 1)
+        def m_part(h, c, i):
+            def emit():
+                for g in range(M_PASSES):
+                    columns = slice(i * P, (i + 1) * P)
+                    mx(sums["out", h, c, i], ("mn", h, g), columns, ("wm", g, c), False, g == M_PASSES - 1)
 
-        def EV(kind, h, g, b):
-            xt = xts[kind, h, g, b]
-            if kind == "m":
-                if b == 0:
-                    grp["m", h, g] = work.tile([P, W, PACK], BF16, name="mg", tag="mg", bufs=MGB, align_bytes=64)
-                words = grp["m", h, g][:].rearrange("p n j -> p (n j)").bitcast(F32)
-                nc.scalar.copy(
-                    out=words[:, b * W : (b + 1) * W].rearrange("p (i r u) -> p i r u", i=2, u=2),
-                    in_=xt[:].rearrange("p i u r -> p i r u"),
-                )
-            else:
-                if b == 0:
-                    pln["z", h, g] = work.tile([P, 2, W], F32, name="zp", tag="zp", bufs=ZPB, align_bytes=64)
-                nc.scalar.copy(
-                    out=pln["z", h, g][:, :, b * 256 : (b + 1) * 256].rearrange("p u (i r) -> p u i r", i=2),
-                    in_=xt[:].rearrange("p i u r -> p u i r"),
-                )
+            needs = [("quantise", "mn", h, g) for g in range(M_PASSES)]
+            needs += [("quantise", "wm", g, c) for g in range(M_PASSES)]
+            task("tensor", ("m_part", h, c, i), needs + [("z_part", h, c, i)], emit)
 
-        def UE(h):
-            u_sb[h] = keep.tile([P, W], F32, name="u%d" % h, tag="u%d" % h)
-            nc.scalar.copy(out=u_sb[h][:], in_=accs["u", h][:])
+        def finish(h, c, i):
+            def emit():
+                res = work.tile([P, W], F32, name="res", tag="res", bufs=4)
+                nc.scalar.activation(out=res[:], in_=sums["out", h, c, i][:], func=ACT.Tanh)
+                nc.sync.dma_start(out=out_dst[h, i][:, c * W : (c + 1) * W], in_=res[:])
 
-        def WZ(g, c):
-            planar = work.tile([P, PACK, W], BF16, name="wzp", tag="wzp", bufs=3, align_bytes=64)
-            for t in range(PACK):
-                nc.scalar.activation(
-                    out=planar[:, t, :],
-                    in_=wz_raw[g][:, t, c * W : (c + 1) * W].bitcast(FP8),
-                    func=ACT.Copy,
-                    scale=sc_sb[:, g, t : t + 1],
-                )
-            pln["wz", g, c] = planar
+            task("scalar", ("finish", h, c, i), [("m_part", h, c, i)], emit)
 
-        def OUT(h, i, c):
-            res = work.tile([P, W], F32, name="res", tag="res", bufs=4)
-            nc.scalar.activation(out=res[:], in_=accs["o", h, i, c][:], func=ACT.Tanh)
-            nc.sync.dma_start(out=out[(h * 4 + i) * P : (h * 4 + i + 1) * P, c * W : (c + 1) * W], in_=res[:])
+        def warm(kind, a, b):
+            def emit():
+                acc = psum.tile([P, W], F32, name="sums", tag="sums", bufs=SUM_BANKS)
+                src = raw["at", a][:, 0, 0:W] if kind == "at" else raw[kind, a, b][:, 0:W]
+                for r in range(2):
+                    nc.tensor.matmul(acc[:], lhsT=zeros[:], rhs=src, start=True, stop=True)
 
-        def wgroup(e):
-            tag = "wg" + e
-            return work.tile([P, W, PACK], BF16, name=tag, tag=tag, bufs=3 if e == "V" else 2, align_bytes=64)
+            load = ("load", "at", a) if kind == "at" else ("load", kind, a, b // 2)
+            key = ("warm", kind, a, b)
+            task("tensor", key, [load] + buffer("sums", SUM_BANKS, [key]), emit)
 
-        def ATI(g, c, e):
-            grp["at", g, c] = wgroup(e)
-            copy_on(
-                e,
-                grp["at", g, c][:].rearrange("p (t q) j -> p t q j", t=PACK),
-                at_raw[g, c][:].rearrange("p j (q t) -> p t q j", t=PACK),
-            )
 
-        def WMI(g, c, e):
-            grp["wm", g, c] = wgroup(e)
-            interleave(e, grp["wm", g, c][:], wm_raw[g, c][:])
+        for b in range(2):
+            load_rows("m", 0, b)
+        load_weight("at", 0)
+        for b in range(2):
+            load_rows("z", 0, b)
+        load_wz(0)
+        load_vectors()
+        load_rows("m", 1, 0)
+        load_weight("at", 1)
+        load_wz(1)
+        load_rows("m", 1, 1)
+        load_rows("z", 1, 0)
+        load_wz(2)
+        load_rows("z", 1, 1)
+        for g in range(M_PASSES):
+            load_weight("wm", g)
 
-        def WZI(g, c, e):
-            grp["wz", g, c] = wgroup(e)
-            interleave(e, grp["wz", g, c][:], pln["wz", g, c][:])
+        z_banks = [(g, b) for g in range(Z_PASSES) for b in range(2)]
+        warm("m", 0, 0)
+        warm("m", 0, 2)
+        for g in range(M_PASSES):
+            turn("m", 0, g, 0)
+        warm("at", 0, 0)
+        for g in range(M_PASSES):
+            turn("m", 0, g, 1)
+        turn("z", 0, 0, 0)
+        warm("z", 0, 0)
+        for g, b in z_banks[1:5]:
+            turn("z", 0, g, b)
+        warm("z", 0, 2)
+        turn("z", 0, 2, 1)
+        turn("m", 1, 0, 0)
+        dot(0, 0)
+        turn("m", 1, 1, 0)
+        dot(0, 1)
+        dot(0, 2)
+        turn("m", 1, 0, 1)
+        for t in range(PACK):
+            step(0, 0, t)
+        turn("m", 1, 1, 1)
+        for t, banks in ((0, z_banks[0:1]), (1, z_banks[1:3]), (2, z_banks[3:5])):
+            step(0, 1, t)
+            for g, b in banks:
+                turn("z", 1, g, b)
+        dot(1, 0)
+        turn("z", 1, 2, 1)
+        step(0, 1, 3)
+        dot(1, 1)
+        dot(1, 2)
+        for t in range(3):
+            step(1, 0, t)
+        z_part(0, 0, 0)
+        z_part(0, 0, 1)
+        step(1, 0, 3)
+        step(1, 1, 0)
+        m_part(0, 0, 0)
+        step(1, 1, 1)
+        m_part(0, 0, 1)
+        z_part(0, 0, 2)
+        step(1, 1, 2)
+        step(1, 1, 3)
+        m_part(0, 0, 2)
+        for i in range(3):
+            z_part(1, 0, i)
+        z_part(0, 0, 3)
+        m_part(0, 0, 3)
+        z_part(1, 0, 3)
+        for i in range(4):
+            m_part(1, 0, i)
+        for pair in ((0, 1), (2, 3)):
+            for part in (z_part, m_part):
+                for h in range(HALVES):
+                    for i in pair:
+                        part(h, 1, i)
 
-        def ZI(h, g):
-            grp["z", h, g] = work.tile([P, W, PACK], BF16, name="zg", tag="zg", bufs=2, align_bytes=64)
-            nc.vector.tensor_copy(
-                out=grp["z", h, g][:].rearrange("p n j -> p (n j)").bitcast(F32).rearrange("p (n u) -> p n u", u=2),
-                in_=pln["z", h, g][:].rearrange("p u n -> p n u"),
-            )
+        for b in range(2):
+            for g in range(M_PASSES):
+                empty("m", 0, g, b)
+        for g, b in z_banks[0:4]:
+            empty("z", 0, g, b)
+        widen(0, 0)
+        for g, b in z_banks[4:6]:
+            empty("z", 0, g, b)
+        empty("m", 1, 0, 0)
+        widen(1, 0)
+        empty("m", 1, 1, 0)
+        keep_u(0)
+        widen(2, 0)
+        interleave("scalar", "wz", 1, 0)
+        for g in range(M_PASSES):
+            empty("m", 1, g, 1)
+        for g, b in z_banks[0:2]:
+            empty("z", 1, g, b)
+        widen(0, 1)
+        for g, b in z_banks[2:6]:
+            empty("z", 1, g, b)
+        widen(1, 1)
+        keep_u(1)
+        interleave("scalar", "mn", 0, 1)
+        widen(2, 1)
+        finish(0, 0, 0)
+        finish(0, 0, 1)
+        interleave("scalar", "mn", 1, 0)
+        finish(0, 0, 2)
+        interleave("scalar", "mn", 1, 1)
+        interleave("scalar", "wz", 2, 1)
+        finish(0, 0, 3)
+        for i in range(4):
+            finish(1, 0, i)
+        for pair in ((0, 1), (2, 3)):
+            for h in range(HALVES):
+                for i in pair:
+                    finish(h, 1, i)
 
-        def STT(h, c, t):
-            if t == 0:
-                pln["mn", h, c] = work.tile([P, PACK, W], BF16, name="mnp", tag="mnp", bufs=3, align_bytes=64)
-            nc.vector.scalar_tensor_tensor(
-                out=pln["mn", h, c][:, t, :],
-                in0=u_sb[h][:],
-                scalar=bv_sb[:, c, t : t + 1],
-                in1=accs["s", h, c, t][:],
-                op0=ALU.mult,
-                op1=ALU.add,
-            )
+        interleave("vector", "at", 0, 0)
+        interleave("vector", "at", 0, 1)
+        quantise("m", 0, 0)
+        quantise("at", 0, 0)
+        quantise("m", 0, 1)
+        group(0, 0)
+        quantise("at", 0, 1)
+        group(0, 1)
+        quantise("z", 0, 0)
+        quantise("z", 0, 1)
+        interleave("vector", "wz", 0, 0)
+        interleave("vector", "at", 1, 0)
+        interleave("vector", "at", 1, 1)
+        quantise("at", 1, 0)
+        quantise("wz", 0, 0)
+        quantise("at", 1, 1)
+        add(0, 0, 0)
+        group(0, 2)
+        for t in range(1, PACK):
+            add(0, 0, t)
+        interleave("vector", "wz", 2, 0)
+        quantise("z", 0, 2)
+        interleave("vector", "wm", 0, 0)
+        add(0, 1, 0)
+        quantise("wm", 0, 0)
+        quantise("wz", 1, 0)
+        interleave("vector", "wm", 1, 0)
+        interleave("vector", "mn", 0, 0)
+        add(0, 1, 1)
+        add(0, 1, 2)
+        for g in range(M_PASSES):
+            quantise("m", 1, g)
+        add(0, 1, 3)
+        quantise("wz", 2, 0)
+        quantise("mn", 0, 0)
+        add(1, 0, 0)
+        add(1, 0, 1)
+        quantise("wm", 1, 0)
+        group(1, 0)
+        quantise("mn", 0, 1)
+        add(1, 0, 2)
+        add(1, 0, 3)
+        add(1, 1, 0)
+        quantise("z", 1, 0)
+        group(1, 1)
+        group(1, 2)
+        add(1, 1, 1)
+        quantise("z", 1, 1)
+        quantise("z", 1, 2)
+        add(1, 1, 2)
+        add(1, 1, 3)
+        interleave("vector", "wz", 0, 1)
+        quantise("mn", 1, 0)
+        quantise("wz", 0, 1)
+        quantise("mn", 1, 1)
+        interleave("vector", "wz", 1, 1)
+        quantise("wz", 1, 1)
+        quantise("wz", 2, 1)
+        for g in range(M_PASSES):
+            interleave("vector", "wm", g, 1)
+        for g in range(M_PASSES):
+            quantise("wm", g, 1)
 
-        def MNI(h, c, e):
-            tag = "mng" + e
-            grp["mn", h, c] = work.tile([P, W, PACK], BF16, name=tag, tag=tag, bufs=2, align_bytes=64)
-            interleave(e, grp["mn", h, c][:], pln["mn", h, c][:])
-
-        def Q(*key):
-            name = "".join(str(k) for k in (("m",) + key[1:] if key[0] == "mn" else key))
-            codes[key] = codes_tile(name)
-            quantize(codes[key], grp[key])
-        def dispatch(key):
-            kind = key[0]
-            if kind == "LD":
-                if key[1] == "at":
-                    load_w(at_raw, at_src, key[2], key[3])
-                elif key[1] == "wm":
-                    load_w(wm_raw, wm_src, key[2], key[3])
-                elif key[1] == "m":
-                    load_m(key[2])
-                elif key[1] == "z":
-                    load_z(key[2])
-                elif key[1] == "wz":
-                    load_wz(key[2])
-                else:
-                    nc.sync.dma_start(out=ez_sb[:], in_=ez.rearrange("(g p j) -> p g j", p=P, j=PACK))
-                    nc.sync.dma_start(out=bv_sb[:], in_=bvec.rearrange("(g p j) -> p g j", p=P, j=PACK))
-                    nc.sync.dma_start(out=sc_sb[:], in_=wz_scale.rearrange("(g p j) o -> p g (j o)", p=P, j=PACK))
-            else:
-                FN[kind](*key[1:])
-
-        FN = {"T": T, "U": U, "S1": S1, "ZW": ZW, "MW": MW, "EV": EV, "UE": UE, "WZ": WZ, "OUT": OUT, "ATI": ATI,
-              "WMI": WMI, "WZI": WZI, "ZI": ZI, "STT": STT, "MNI": MNI, "Q": Q}
-
+        done = set()
+        heads = {name: 0 for name in queues}
         with tc.manual_schedule():
-            for key in ORDER:
-                dispatch(key)
+            while any(heads[name] < len(queues[name]) for name in queues):
+                before = len(done)
+                for name in queues:
+                    while heads[name] < len(queues[name]):
+                        key, needs, emit = queues[name][heads[name]]
+                        if not all(need in done for need in needs):
+                            break
+                        emit()
+                        done.add(key)
+                        heads[name] += 1
+                assert len(done) > before

from contextlib import ExitStack

import concourse.mybir as mybir
from concourse.masks import make_identity

N, K, MEM, H = 1024, 1536, 1024, 1024
FLOPS = 2 * N * (K * H + MEM * MEM + MEM * H) + 2 * N * K + 3 * N * MEM

F32 = mybir.dt.float32
BF16 = mybir.dt.bfloat16
U32 = mybir.dt.uint32
U8 = mybir.dt.uint8
FP8 = mybir.dt.float8_e4m3fn
FP8X4 = mybir.dt.float8_e4m3fn_x4
ACT = mybir.ActivationFunctionType
ALU = mybir.AluOpType

P = 128
PACK = 4
PASS = P * PACK
W = 512
Z_PASSES = K // PASS
M_PASSES = MEM // PASS
HALVES = 2

TURN_BANKS = 3
SUM_BANKS = 5
GROUPED_V = 6
GROUPED_S = 5


def tile_legendrememoryunitstep_kernel(tc, z, m, ez, at, bvec, wz_bytes, wz_scale, wm, out):
    nc = tc.nc
    with ExitStack() as ctx:
        keep = ctx.enter_context(tc.tile_pool(name="keep", bufs=1))
        work = ctx.enter_context(tc.tile_pool(name="work", bufs=1))
        psum = ctx.enter_context(tc.psum_pool(name="psum", bufs=1))

        row_src = {
            "m": m.rearrange("(h p i) k -> h p i k", h=HALVES, p=P),
            "z": z.rearrange("(h p i) k -> h p i k", h=HALVES, p=P),
        }
        out_dst = out.rearrange("(h p i) k -> h i p k", h=HALVES, p=P)
        weight_src = {
            "at": at.rearrange("(g p j) w -> g p j w", p=P, j=PACK),
            "wm": wm.rearrange("(g p j) w -> g p j w", p=P, j=PACK),
        }
        wz_src = wz_bytes.rearrange("(g p j) w -> g p j w", p=P, j=PACK)

        spark = keep.tile([P, 2], F32, name="spark")
        nc.vector.memset(spark[:], 0.0)
        nc.scalar.activation(out=spark[:, 1:2], in_=spark[:, 0:1], func=ACT.Tanh)
        ident = keep.tile([P, P], F32, name="ident")
        make_identity(nc, ident[:])
        zeros = keep.tile([P, P], BF16, name="zeros")
        nc.vector.memset(zeros[:], 0.0)
        ez_sb = keep.tile([P, Z_PASSES, PACK], BF16, name="ez_sb")
        bvec_sb = keep.tile([P, M_PASSES, PACK], BF16, name="bvec_sb")
        scale_sb = keep.tile([P, Z_PASSES, PACK], F32, name="scale_sb")

        queues = {"sync": [], "tensor": [], "scalar": [], "vector": []}
        rings = {}
        raw, turned, words, planar, grouped, codes, sums, u_sb = {}, {}, {}, {}, {}, {}, {}, {}

        def task(queue, key, needs, emit):
            queues[queue].append((key, needs, emit))

        def buffer(ring, bufs, last_readers):
            uses = rings.setdefault(ring, [])
            uses.append(last_readers)
            return uses[-1 - bufs] if len(uses) > bufs else []

        def engine_of(queue):
            return nc.vector.tensor_copy if queue == "vector" else nc.scalar.copy


        def load_rows(kind, h, b):
            def emit():
                tag = kind + "_raw"
                t = work.tile([P, 2, MEM if kind == "m" else K], BF16, name=tag, tag=tag, bufs=3)
                nc.sync.dma_start(out=t[:], in_=row_src[kind][h][:, 2 * b : 2 * b + 2, :])
                for i in range(2):
                    raw[kind, h, 2 * b + i] = t[:, i, :]

            last_pass = (M_PASSES if kind == "m" else Z_PASSES) - 1
            task("sync", ("load", kind, h, b), buffer(kind + "_raw", 3, [("turn", kind, h, last_pass, b)]), emit)

        def load_weight(kind, g):
            def emit():
                raw[kind, g] = work.tile([P, PACK, H], BF16, name="w_raw", tag="w_raw", bufs=3)
                nc.sync.dma_start(out=raw[kind, g][:], in_=weight_src[kind][g])

            readers = [("interleave", kind, g, c) for c in range(HALVES)]
            task("sync", ("load", kind, g), buffer("w_raw", 3, readers), emit)

        def load_wz(g):
            def emit():
                raw["wz", g] = work.tile([P, PACK, H], U8, name="wz_raw", tag="wz_raw", bufs=Z_PASSES)
                nc.sync.dma_start(out=raw["wz", g][:], in_=wz_src[g])

            task("sync", ("load", "wz", g), [], emit)

        def load_vectors():
            def emit():
                nc.sync.dma_start(out=ez_sb[:], in_=ez.rearrange("(g p j) -> p g j", p=P, j=PACK))
                nc.sync.dma_start(out=bvec_sb[:], in_=bvec.rearrange("(g p j) -> p g j", p=P, j=PACK))
                nc.sync.dma_start(out=scale_sb[:], in_=wz_scale.rearrange("(g p j) o -> p g (j o)", p=P, j=PACK))

            task("sync", ("load", "vectors"), [], emit)


        def turn(kind, h, g, b):
            def emit():
                bank = psum.tile([P, 2, 2, P], F32, name="turned", tag="turned", bufs=TURN_BANKS)
                for i in range(2):
                    src = raw[kind, h, 2 * b + i].bitcast(F32)
                    for u in range(2):
                        nc.tensor.transpose(
                            bank[:, i, u, :], src[:, 256 * g + u : 256 * (g + 1) : 2], ident[:]
                        )
                turned[kind, h, g, b] = bank

            free = buffer("turned", TURN_BANKS, [("empty", kind, h, g, b)])
            task("tensor", ("turn", kind, h, g, b), [("load", kind, h, b)] + free, emit)

        def empty(kind, h, g, b):
            def emit():
                src = turned[kind, h, g, b][:]
                if kind == "m":
                    if b == 0:
                        grouped["m", h, g] = work.tile(
                            [P, W, PACK], BF16, name="grouped_s", tag="grouped_s", bufs=GROUPED_S, align_bytes=64
                        )
                    dst = grouped["m", h, g][:].rearrange("p n j -> p (n j)").bitcast(F32)
                    nc.scalar.copy(
                        out=dst[:, b * W : (b + 1) * W].rearrange("p (i r u) -> p i r u", i=2, u=2),
                        in_=src.rearrange("p i u r -> p i r u"),
                    )
                else:
                    if b == 0:
                        words[h, g] = work.tile([P, 2, W], F32, name="z_words", tag="z_words", bufs=4)
                    nc.scalar.copy(
                        out=words[h, g][:, :, b * 256 : (b + 1) * 256].rearrange("p u (i r) -> p u i r", i=2),
                        in_=src.rearrange("p i u r -> p u i r"),
                    )

            free = []
            if b == 0 and kind == "m":
                free = buffer("grouped_s", GROUPED_S, [("quantise", "m", h, g)])
            elif b == 0:
                free = buffer("z_words", 4, [("group", h, g), ("dot", h, g)])
            task("scalar", ("empty", kind, h, g, b), [("turn", kind, h, g, b)] + free, emit)

        def group(h, g):
            def emit():
                t = work.tile([P, W, PACK], BF16, name="grouped_v", tag="grouped_v", bufs=GROUPED_V, align_bytes=64)
                nc.vector.tensor_copy(
                    out=t[:].rearrange("p n j -> p (n j)").bitcast(F32).rearrange("p (n u) -> p n u", u=2),
                    in_=words[h, g][:].rearrange("p u n -> p n u"),
                )
                grouped["z", h, g] = t

            free = buffer("grouped_v", GROUPED_V, [("quantise", "z", h, g)])
            task("vector", ("group", h, g), [("empty", "z", h, g, b) for b in range(2)] + free, emit)


        def dot(h, g):
            def emit():
                if g == 0:
                    sums["u", h] = psum.tile([P, W], F32, name="sums", tag="sums", bufs=SUM_BANKS)
                for t in range(PACK):
                    nc.tensor.matmul(
                        sums["u", h][:],
                        lhsT=ez_sb[:, g, t : t + 1].to_broadcast([P, P]),
                        rhs=words[h, g][:, t // 2, :].bitcast(BF16)[:, t % 2 : 2 * W : 2],
                        start=(g == 0 and t == 0),
                        stop=(g == Z_PASSES - 1 and t == PACK - 1),
                    )

            free = buffer("sums", SUM_BANKS, [("keep_u", h)]) if g == 0 else [("dot", h, g - 1)]
            needs = [("load", "vectors")] + [("empty", "z", h, g, b) for b in range(2)]
            task("tensor", ("dot", h, g), needs + free, emit)

        def keep_u(h):
            def emit():
                u_sb[h] = keep.tile([P, W], F32, name="u%d" % h)
                nc.scalar.copy(out=u_sb[h][:], in_=sums["u", h][:])

            task("scalar", ("keep_u", h), [("dot", h, Z_PASSES - 1)], emit)


        def interleave(queue, kind, a, b):
            def emit():
                tag = "grouped_" + queue[0]
                bufs = GROUPED_V if queue == "vector" else GROUPED_S
                dst = work.tile([P, W, PACK], BF16, name=tag, tag=tag, bufs=bufs, align_bytes=64)
                copy = engine_of(queue)
                if kind == "at":
                    src = raw["at", a][:, :, b * W : (b + 1) * W]
                    for t in range(PACK):
                        copy(
                            out=dst[:, t * P : (t + 1) * P, :].rearrange("p (c i) j -> p c j i", i=4),
                            in_=src[:, :, t : W : PACK].rearrange("p j (c i) -> p c j i", i=4),
                        )
                else:
                    src = raw["wm", a][:, :, b * W : (b + 1) * W] if kind == "wm" else planar[kind, a, b][:]
                    copy(
                        out=dst[:].rearrange("p (c i) j -> p c j i", i=4),
                        in_=src.rearrange("p j (c i) -> p c j i", i=4),
                    )
                grouped[kind, a, b] = dst

            if kind == "mn":
                needs = [("add", a, b, PACK - 1)]
            elif kind == "wz":
                needs = [("widen", a, b)]
            else:
                needs = [("load", kind, a)]
            tag = "grouped_" + queue[0]
            free = buffer(tag, GROUPED_V if queue == "vector" else GROUPED_S, [("quantise", kind, a, b)])
            task(queue, ("interleave", kind, a, b), needs + free, emit)

        def widen(g, c):
            def emit():
                t = work.tile([P, PACK, W], BF16, name="wz_planar", tag="wz_planar", bufs=3)
                for j in range(PACK):
                    nc.scalar.activation(
                        out=t[:, j, :],
                        in_=raw["wz", g][:, j, c * W : (c + 1) * W].bitcast(FP8),
                        func=ACT.Copy,
                        scale=scale_sb[:, g, j : j + 1],
                    )
                planar["wz", g, c] = t

            free = buffer("wz_planar", 3, [("interleave", "wz", g, c)])
            task("scalar", ("widen", g, c), [("load", "wz", g), ("load", "vectors")] + free, emit)

        def quantise(kind, a, b):
            def emit():
                name = "%s%d%d" % (kind, a, b)
                word = keep.tile([P, W], U32, name=name + "_codes", align_bytes=64)
                scale = keep.tile([P, W], U8, name=name + "_scales", align_bytes=64)
                nc.vector.quantize_mx(
                    out=word[:].bitcast(FP8X4),
                    scales=scale[:],
                    in_=grouped[kind, a, b][:].rearrange("p n j -> p (n j)"),
                )
                codes[kind, a, b] = (word, scale)

            if kind == "m":
                needs = [("empty", "m", a, b, 1)]
            elif kind == "z":
                needs = [("group", a, b)]
            else:
                needs = [("interleave", kind, a, b)]
            task("vector", ("quantise", kind, a, b), needs, emit)


        def mx(acc, lhs, columns, rhs, start, stop):
            nc.tensor.matmul_mx(
                out=acc[:],
                lhsT=codes[lhs][0][:, columns].bitcast(FP8X4),
                lhsT_scale=codes[lhs][1][:, columns],
                rhs=codes[rhs][0][:].bitcast(FP8X4),
                rhs_scale=codes[rhs][1][:],
                start=start,
                stop=stop,
            )

        def step(h, c, t):
            def emit():
                sums["mn", h, c, t] = psum.tile([P, W], F32, name="sums", tag="sums", bufs=SUM_BANKS)
                for g in range(M_PASSES):
                    columns = slice(t * P, (t + 1) * P)
                    mx(sums["mn", h, c, t], ("at", g, c), columns, ("m", h, g), g == 0, g == M_PASSES - 1)

            needs = [("quantise", "at", g, c) for g in range(M_PASSES)]
            needs += [("quantise", "m", h, g) for g in range(M_PASSES)]
            task("tensor", ("step", h, c, t), needs + buffer("sums", SUM_BANKS, [("add", h, c, t)]), emit)

        def add(h, c, t):
            def emit():
                if t == 0:
                    planar["mn", h, c] = work.tile([P, PACK, W], BF16, name="mn_planar", tag="mn_planar", bufs=3)
                nc.vector.scalar_tensor_tensor(
                    out=planar["mn", h, c][:, t, :],
                    in0=u_sb[h][:],
                    scalar=bvec_sb[:, c, t : t + 1],
                    in1=sums["mn", h, c, t][:],
                    op0=ALU.mult,
                    op1=ALU.add,
                )

            free = buffer("mn_planar", 3, [("interleave", "mn", h, c)]) if t == 0 else []
            task("vector", ("add", h, c, t), [("step", h, c, t), ("keep_u", h)] + free, emit)

        def z_part(h, c, i):
            def emit():
                sums["out", h, c, i] = psum.tile([P, W], F32, name="sums", tag="sums", bufs=SUM_BANKS)
                for g in range(Z_PASSES):
                    columns = slice(i * P, (i + 1) * P)
                    mx(sums["out", h, c, i], ("z", h, g), columns, ("wz", g, c), g == 0, False)

            needs = [("quantise", "z", h, g) for g in range(Z_PASSES)]
            needs += [("quantise", "wz", g, c) for g in range(Z_PASSES)]
            task("tensor", ("z_part", h, c, i), needs + buffer("sums", SUM_BANKS, [("finish", h, c, i)]), emit)

        def m_part(h, c, i):
            def emit():
                for g in range(M_PASSES):
                    columns = slice(i * P, (i + 1) * P)
                    mx(sums["out", h, c, i], ("mn", h, g), columns, ("wm", g, c), False, g == M_PASSES - 1)

            needs = [("quantise", "mn", h, g) for g in range(M_PASSES)]
            needs += [("quantise", "wm", g, c) for g in range(M_PASSES)]
            task("tensor", ("m_part", h, c, i), needs + [("z_part", h, c, i)], emit)

        def finish(h, c, i):
            def emit():
                res = work.tile([P, W], F32, name="res", tag="res", bufs=4)
                nc.scalar.activation(out=res[:], in_=sums["out", h, c, i][:], func=ACT.Tanh)
                nc.sync.dma_start(out=out_dst[h, i][:, c * W : (c + 1) * W], in_=res[:])

            task("scalar", ("finish", h, c, i), [("m_part", h, c, i)], emit)

        def warm(kind, a, b):
            def emit():
                acc = psum.tile([P, W], F32, name="sums", tag="sums", bufs=SUM_BANKS)
                src = raw["at", a][:, 0, 0:W] if kind == "at" else raw[kind, a, b][:, 0:W]
                for r in range(2):
                    nc.tensor.matmul(acc[:], lhsT=zeros[:], rhs=src, start=True, stop=True)

            load = ("load", "at", a) if kind == "at" else ("load", kind, a, b // 2)
            key = ("warm", kind, a, b)
            task("tensor", key, [load] + buffer("sums", SUM_BANKS, [key]), emit)


        for b in range(2):
            load_rows("m", 0, b)
        load_weight("at", 0)
        for b in range(2):
            load_rows("z", 0, b)
        load_wz(0)
        load_vectors()
        load_rows("m", 1, 0)
        load_weight("at", 1)
        load_wz(1)
        load_rows("m", 1, 1)
        load_rows("z", 1, 0)
        load_wz(2)
        load_rows("z", 1, 1)
        for g in range(M_PASSES):
            load_weight("wm", g)

        z_banks = [(g, b) for g in range(Z_PASSES) for b in range(2)]
        warm("m", 0, 0)
        warm("m", 0, 2)
        for g in range(M_PASSES):
            turn("m", 0, g, 0)
        warm("at", 0, 0)
        for g in range(M_PASSES):
            turn("m", 0, g, 1)
        turn("z", 0, 0, 0)
        warm("z", 0, 0)
        for g, b in z_banks[1:5]:
            turn("z", 0, g, b)
        warm("z", 0, 2)
        turn("z", 0, 2, 1)
        turn("m", 1, 0, 0)
        dot(0, 0)
        turn("m", 1, 1, 0)
        dot(0, 1)
        dot(0, 2)
        turn("m", 1, 0, 1)
        for t in range(PACK):
            step(0, 0, t)
        turn("m", 1, 1, 1)
        for t, banks in ((0, z_banks[0:1]), (1, z_banks[1:3]), (2, z_banks[3:5])):
            step(0, 1, t)
            for g, b in banks:
                turn("z", 1, g, b)
        dot(1, 0)
        turn("z", 1, 2, 1)
        step(0, 1, 3)
        dot(1, 1)
        dot(1, 2)
        for t in range(3):
            step(1, 0, t)
        z_part(0, 0, 0)
        z_part(0, 0, 1)
        step(1, 0, 3)
        step(1, 1, 0)
        m_part(0, 0, 0)
        step(1, 1, 1)
        m_part(0, 0, 1)
        z_part(0, 0, 2)
        step(1, 1, 2)
        step(1, 1, 3)
        m_part(0, 0, 2)
        for i in range(3):
            z_part(1, 0, i)
        z_part(0, 0, 3)
        m_part(0, 0, 3)
        z_part(1, 0, 3)
        for i in range(4):
            m_part(1, 0, i)
        for pair in ((0, 1), (2, 3)):
            for part in (z_part, m_part):
                for h in range(HALVES):
                    for i in pair:
                        part(h, 1, i)

        for b in range(2):
            for g in range(M_PASSES):
                empty("m", 0, g, b)
        for g, b in z_banks[0:4]:
            empty("z", 0, g, b)
        widen(0, 0)
        for g, b in z_banks[4:6]:
            empty("z", 0, g, b)
        empty("m", 1, 0, 0)
        widen(1, 0)
        empty("m", 1, 1, 0)
        keep_u(0)
        widen(2, 0)
        interleave("scalar", "wz", 1, 0)
        for g in range(M_PASSES):
            empty("m", 1, g, 1)
        for g, b in z_banks[0:2]:
            empty("z", 1, g, b)
        widen(0, 1)
        for g, b in z_banks[2:6]:
            empty("z", 1, g, b)
        widen(1, 1)
        keep_u(1)
        interleave("scalar", "mn", 0, 1)
        widen(2, 1)
        finish(0, 0, 0)
        finish(0, 0, 1)
        interleave("scalar", "mn", 1, 0)
        finish(0, 0, 2)
        interleave("scalar", "mn", 1, 1)
        interleave("scalar", "wz", 2, 1)
        finish(0, 0, 3)
        for i in range(4):
            finish(1, 0, i)
        for pair in ((0, 1), (2, 3)):
            for h in range(HALVES):
                for i in pair:
                    finish(h, 1, i)

        interleave("vector", "at", 0, 0)
        interleave("vector", "at", 0, 1)
        quantise("m", 0, 0)
        quantise("at", 0, 0)
        quantise("m", 0, 1)
        group(0, 0)
        quantise("at", 0, 1)
        group(0, 1)
        quantise("z", 0, 0)
        quantise("z", 0, 1)
        interleave("vector", "wz", 0, 0)
        interleave("vector", "at", 1, 0)
        interleave("vector", "at", 1, 1)
        quantise("at", 1, 0)
        quantise("wz", 0, 0)
        quantise("at", 1, 1)
        add(0, 0, 0)
        group(0, 2)
        for t in range(1, PACK):
            add(0, 0, t)
        interleave("vector", "wz", 2, 0)
        quantise("z", 0, 2)
        interleave("vector", "wm", 0, 0)
        add(0, 1, 0)
        quantise("wm", 0, 0)
        quantise("wz", 1, 0)
        interleave("vector", "wm", 1, 0)
        interleave("vector", "mn", 0, 0)
        add(0, 1, 1)
        add(0, 1, 2)
        for g in range(M_PASSES):
            quantise("m", 1, g)
        add(0, 1, 3)
        quantise("wz", 2, 0)
        quantise("mn", 0, 0)
        add(1, 0, 0)
        add(1, 0, 1)
        quantise("wm", 1, 0)
        group(1, 0)
        quantise("mn", 0, 1)
        add(1, 0, 2)
        add(1, 0, 3)
        add(1, 1, 0)
        quantise("z", 1, 0)
        group(1, 1)
        group(1, 2)
        add(1, 1, 1)
        quantise("z", 1, 1)
        quantise("z", 1, 2)
        add(1, 1, 2)
        add(1, 1, 3)
        interleave("vector", "wz", 0, 1)
        quantise("mn", 1, 0)
        quantise("wz", 0, 1)
        quantise("mn", 1, 1)
        interleave("vector", "wz", 1, 1)
        quantise("wz", 1, 1)
        quantise("wz", 2, 1)
        for g in range(M_PASSES):
            interleave("vector", "wm", g, 1)
        for g in range(M_PASSES):
            quantise("wm", g, 1)

        done = set()
        heads = {name: 0 for name in queues}
        with tc.manual_schedule():
            while any(heads[name] < len(queues[name]) for name in queues):
                before = len(done)
                for name in queues:
                    while heads[name] < len(queues[name]):
                        key, needs, emit = queues[name][heads[name]]
                        if not all(need in done for need in needs):
                            break
                        emit()
                        done.add(key)
                        heads[name] += 1
                assert len(done) > before
